import numpy as np
import ml_dtypes


def mxq(x, axis, fmt="e4m3"):
    dtype, down = {"e4m3": (ml_dtypes.float8_e4m3fn, 7), "e5m2": (ml_dtypes.float8_e5m2, 14)}[fmt]
    v = np.moveaxis(np.asarray(x, np.float32).astype(ml_dtypes.bfloat16).astype(np.float64), axis, -1)
    blocks = v.reshape(v.shape[:-1] + (-1, 32))
    amax = np.abs(blocks).max(-1, keepdims=True)
    byte = np.maximum(np.where(amax > 0, np.frexp(amax)[1] - 1 + 127, 0) - down, 1)
    scale = np.exp2(byte - 127.0)
    codes = (blocks / scale).astype(np.float32).astype(dtype).astype(np.float64)
    return np.moveaxis((codes * scale).reshape(v.shape), -1, axis)


WIDE = False


def mx_kscale(k):
    if not WIDE:
        return np.ones(k)
    levels = np.array([10, -10, 5, -5, 0])
    if k % 512:
        return np.exp2(np.random.permutation(np.resize(levels, k // 32))).repeat(32)
    a = np.empty((k // 512, 16))
    for p in range(k // 512):
        a[p, :8] = np.random.permutation(np.resize(levels, 8))
        for g in range(8):
            far = levels[np.abs(levels - a[p, g]) >= 10]
            a[p, g + 8] = far[np.random.randint(len(far))]
    return np.exp2(a.ravel()).repeat(32)


def f64(x):
    return np.asarray(x).astype(np.float64)


def striped(idx):
    return np.tile(idx.reshape(-1, 16).T, (8, 1)).astype(np.uint16)


def unstriped(offs):
    return offs[:16].T.reshape(-1).astype(np.int64)


def pack_weight(w):
    k, n = w.shape
    w = f64(np.asarray(w, np.float32).astype(ml_dtypes.bfloat16)).reshape(k // 32, 32, n)
    amax = np.abs(w).max(1)
    byte = np.clip(np.where(amax > 0, np.frexp(amax)[1] - 1 + 127 - 7, 1), 1, 254)
    scaled = (w * np.exp2(127.0 - byte)[:, None, :]).reshape(k, n).astype(np.float32)
    words = np.ascontiguousarray(scaled.reshape(k // 512, 128, 4, n).transpose(0, 1, 3, 2)).astype(ml_dtypes.float8_e4m3fn).view(np.uint8)
    return words, np.ascontiguousarray(byte.astype(np.uint8).reshape(k // 512, 16, n))


def unpack_weight(words, scales):
    g, p, n, _ = words.shape
    vals = np.ascontiguousarray(words).view(ml_dtypes.float8_e4m3fn).astype(np.float64) * np.repeat(np.exp2(scales.astype(np.float64) - 127.0), 8, axis=1)[..., None]
    return vals.transpose(0, 1, 3, 2).reshape(g * 512, n)


K, T, S, H, N, U = 1024, 2048, 512, 512, 128, 1024


def setup_inputs():
    n = np.random.standard_normal
    s = mx_kscale(K)[:, None]
    u = mx_kscale(H)
    packed_xT = pack_weight(n((K, T)) * s)
    return {
        "x_words": packed_xT[0],
        "x_scales": packed_xT[1],
        "w1": (n((K, H)) / np.sqrt(K) / s * u).astype(np.float32),
        "w2": (n((H, N)) / np.sqrt(H) / u[:, None]).astype(np.float32),
        "skip": (n((H, U)) * u[:, None]).astype(np.float32),
        "offs": striped(np.random.permutation(T)[:S]),
        "cell": striped(np.random.permutation(U)[:S]),
    }


def reference(x_words, x_scales, w1, w2, skip, offs, cell):
    xq = unpack_weight(x_words, x_scales)[:, unstriped(offs)]
    up = np.zeros((H, U))
    up[:, unstriped(cell)] = mxq(f64(w1), 0, "e4m3").T @ xq
    z = up + f64(skip)
    return mxq(f64(w2), 0, "e4m3").T @ mxq(z, 0, "e4m3")

@@ -1,0 +1,238 @@
+from contextlib import ExitStack
+
+import concourse.mybir as mybir
+from concourse.masks import make_identity
+
+K, T, S, H, N, U = 1024, 2048, 512, 512, 128, 1024
+FLOPS = 2 * K * H * S + 2 * H * N * U
+
+F32 = mybir.dt.float32
+BF16 = mybir.dt.bfloat16
+I32 = mybir.dt.int32
+U32 = mybir.dt.uint32
+U16 = mybir.dt.uint16
+U8 = mybir.dt.uint8
+FP8X4 = mybir.dt.float8_e4m3fn_x4
+
+P = 128
+PASSES = 2
+BANK = 512
+QUARTER = 256
+ALIGN = 64
+
+
+def tile_picked_unet_none_p_kernel(tc, x_words, x_scales, w1, w2, skip, offs, cell, out):
+    nc = tc.nc
+    with ExitStack() as ctx:
+        sb = ctx.enter_context(tc.tile_pool(name="sb", bufs=1))
+        ps = ctx.enter_context(tc.psum_pool(name="ps", bufs=1))
+
+        def tile(name, shape, dtype, tag=None):
+            return sb.tile(shape, dtype, name=name, tag=tag or name, align_bytes=ALIGN)
+
+        def bank(name, tag):
+            return ps.tile([P, BANK], F32, name=name, tag=tag)
+
+        offs_t = sb.tile([P, S // 16], U16, name="offs_t")
+        nc.sync.dma_start(offs_t[:], offs)
+        cell_t = sb.tile([P, S // 16], U16, name="cell_t")
+        nc.sync.dma_start(cell_t[:], cell)
+
+        xs = tile("xs", [P, T], U8)
+        nc.gpsimd.memset(xs[:, : T // 2].bitcast(I32), 0)
+        nc.vector.memset(xs[:, T // 2 :].bitcast(I32), 0)
+        xs_dram = x_scales.bitcast(I32)
+        for q in range(4):
+            nc.sync.dma_start(xs[32 * q : 32 * q + 8, :].bitcast(I32), xs_dram[:, 4 * q : 4 * q + 4, :])
+
+        w1_rows = w1.rearrange("(g p j) c -> g p j c", g=PASSES, j=4)
+        raw0 = tile("raw0", [P, PASSES, 4, P], F32)
+        for g in range(PASSES):
+            nc.sync.dma_start(raw0[:, g], w1_rows[g, :, :, 0:P])
+        xw = [tile(f"xw{g}", [P, T], U32) for g in range(PASSES)]
+        for g in range(PASSES):
+            nc.sync.dma_start(xw[g][:].bitcast(I32), x_words[g].rearrange("p n t -> p (n t)").bitcast(I32))
+
+        ident = tile("ident", [P, P], F32)
+        make_identity(nc, ident[:])
+        win = [tile(f"win{w}", [P, U], F32) for w in range(4)]
+        for w in range(4):
+            (nc.vector if w < 2 else nc.gpsimd).memset(win[w][:], 0.0)
+
+        gs = tile("gs", [P, S], U8)
+        nc.vector.tensor_copy(gs[:], xs[:].indirect(offs_t[:]))
+
+        w1_codes, w1_scales = {}, {}
+
+        def quantize_w1_single(w, raw):
+            grouped = tile(f"w1_bf{w}", [P, PASSES * P * 4], BF16)
+            nc.scalar.copy(
+                grouped[:].rearrange("p (g c i j) -> p g c j i", g=PASSES, i=4, j=4),
+                raw[:].rearrange("p g j (c i) -> p g c j i", i=4),
+            )
+            codes = tile(f"w1_codes{w}", [P, PASSES * P], U32)
+            scales = tile(f"w1_scales{w}", [P, PASSES * P], U8)
+            nc.vector.quantize_mx(codes[:].bitcast(FP8X4), scales[:], grouped[:])
+            for g in range(PASSES):
+                w1_codes[w, g] = codes[:, g * P : (g + 1) * P]
+                w1_scales[w, g] = scales[:, g * P : (g + 1) * P]
+
+        quantize_w1_single(0, raw0)
+        raw1 = tile("raw1", [P, PASSES, 4, P], F32, tag="raw0")
+        for g in range(PASSES):
+            nc.sync.dma_start(raw1[:, g], w1_rows[g, :, :, P : 2 * P])
+
+        gw = [tile(f"gw{g}", [P, S], U32) for g in range(PASSES)]
+        nc.vector.tensor_copy(gw[0][:], xw[0][:].indirect(offs_t[:]))
+        for a in (0, S // 2):
+            nc.vector.tensor_copy(gw[1][:, a : a + S // 2], xw[1][:].indirect(offs_t[:, a // 16 : (a + S // 2) // 16]))
+
+        raw23 = [tile(f"raw23_{g}", [P, 4, 2 * P], F32, tag=("w1_bf0", "xw0")[g]) for g in range(PASSES)]
+        for g in range(PASSES):
+            nc.sync.dma_start(raw23[g][:], w1_rows[g, :, :, 2 * P : 4 * P])
+        skip01 = tile("skip01", [P, 2, U], F32, tag="xw1")
+        for w in range(2):
+            nc.sync.dma_start(skip01[:, w, :], skip[w * P : (w + 1) * P, :])
+
+        def h_pass(acc, w, g, a, b, at):
+            nc.tensor.matmul_mx(
+                acc[:, at : at + b - a],
+                lhsT=w1_codes[w, g].bitcast(FP8X4),
+                lhsT_scale=w1_scales[w, g],
+                rhs=gw[g][:, a:b].bitcast(FP8X4),
+                rhs_scale=gs[4 * g :, a:b],
+                start=(g == 0),
+                stop=(g == PASSES - 1),
+            )
+
+        def h_product(w, a, b, tag):
+            acc = bank(f"h{w}_{a}", tag)
+            for lo in range(a, b, QUARTER):
+                for g in range(PASSES):
+                    h_pass(acc, w, g, lo, min(lo + QUARTER, b), lo - a)
+            return acc
+
+        def h_scatter(w, a, b, acc, tag=None, copy=nc.scalar.copy):
+            stage = tile(f"h_sb{w}_{a}", [P, b - a], F32, tag)
+            copy(stage[:], acc[:, : b - a])
+            nc.vector.tensor_copy(win[w][:].indirect(cell_t[:, a // 16 : b // 16]), stage[:])
+
+        half = S // 2
+        acc00 = h_product(0, 0, half, "B0")
+        acc01 = h_product(0, half, S, "B1")
+        h_scatter(0, 0, half, acc00, copy=nc.vector.tensor_copy)
+        quantize_w1_single(1, raw1)
+        h_scatter(0, half, S, acc01, tag="raw0")
+        skip23 = tile("skip23", [P, 2, U], F32, tag="w1_bf1")
+        nc.sync.dma_start(skip23[:], skip[2 * P :, :].rearrange("(p u) v -> p u v", u=2))
+        skips = [skip01[:, 0, :], skip01[:, 1, :], skip23[:, 0, :], skip23[:, 1, :]]
+
+        acc10 = h_product(1, 0, half, "B2")
+        acc11 = h_product(1, half, S, "B3")
+        h_scatter(1, 0, half, acc10)
+        grouped23 = tile("w1_bf23", [P, 2, PASSES, P * 4], BF16)
+        for g in range(PASSES):
+            nc.scalar.copy(
+                grouped23[:, :, g, :].rearrange("p u (c i j) -> p c j i u", i=2, j=4),
+                raw23[g][:].rearrange("p j (c i u) -> p c j i u", i=2, u=2),
+            )
+        codes23 = tile("w1_codes23", [P, 2 * PASSES * P], U32)
+        scales23 = tile("w1_scales23", [P, 2 * PASSES * P], U8)
+        nc.vector.quantize_mx(codes23[:].bitcast(FP8X4), scales23[:], grouped23[:].rearrange("p u g x -> p (u g x)"))
+        for u in range(2):
+            for g in range(PASSES):
+                at = (u * PASSES + g) * P
+                w1_codes[2 + u, g] = codes23[:, at : at + P]
+                w1_scales[2 + u, g] = scales23[:, at : at + P]
+        h_scatter(1, half, S, acc11, tag="xw0")
+        raw_w2 = tile("raw_w2", [P, 4, N], F32, tag="w1_bf23")
+        nc.sync.dma_start(raw_w2[:], w2.rearrange("(p j) n -> p j n", j=4))
+
+        cut = 384
+        acc20 = h_product(2, 0, half, "B0")
+        acc21 = h_product(2, half, S, "B1")
+        acc30 = h_product(3, 0, cut, "B2")
+        h_scatter(2, 0, half, acc20)
+        h_scatter(2, half, S, acc21)
+        h_scatter(3, 0, cut, acc30)
+
+        zt = [tile(f"zt{hf}", [P, 2, 4, 2 * P], BF16) for hf in range(2)]
+
+        def open_sum(w, hf, tag):
+            acc = bank(f"z{w}_{hf}", tag)
+            for c in range(4):
+                cols = slice((4 * hf + c) * P, (4 * hf + c + 1) * P)
+                nc.tensor.matmul(acc[:, c * P : (c + 1) * P], lhsT=skips[w][:, cols], rhs=ident[:],
+                                 is_transpose=True, start=(c == 0), stop=False)
+            return acc
+
+        def close_sum(w, hf, acc):
+            for c in range(4):
+                cols = slice((4 * hf + c) * P, (4 * hf + c + 1) * P)
+                nc.tensor.matmul(acc[:, c * P : (c + 1) * P], lhsT=win[w][:, cols], rhs=ident[:],
+                                 is_transpose=True, start=False, stop=(c == 3))
+
+        def round_sum(w, hf, acc, copy):
+            if w < 2:
+                copy(zt[hf][:, :, :, 64 * w : 64 * (w + 1)], acc[:].rearrange("p (c x u) -> p u c x", c=4, u=2))
+            else:
+                copy(zt[hf][:, w - 2, :, P:], acc[:].rearrange("p (c x) -> p c x", c=4))
+
+        sums = {}
+        for w, tag in ((0, "A"), (1, "C")):
+            for hf in range(2):
+                sums[w, hf] = open_sum(w, hf, f"{tag}{hf}")
+            for hf in range(2):
+                close_sum(w, hf, sums[w, hf])
+                round_sum(w, hf, sums[w, hf], nc.scalar.copy)
+        for hf in range(2):
+            sums[3, hf] = open_sum(3, hf, f"A{hf}")
+        for hf in range(2):
+            sums[2, hf] = open_sum(2, hf, f"C{hf}")
+        for hf in range(2):
+            close_sum(2, hf, sums[2, hf])
+            round_sum(2, hf, sums[2, hf], nc.scalar.copy)
+
+        acc31 = h_product(3, cut, S, "C0")
+        h_scatter(3, cut, S, acc31, tag="last")
+
+        back = [bank(f"back{q}", f"B{q}") for q in range(4)]
+
+        def turn_back(q, u):
+            for c in range(2):
+                words = zt[q // 2][:, u, 2 * (q % 2) + c, :].bitcast(F32)
+                at = u * QUARTER + c * P
+                nc.tensor.transpose(back[q][:, at : at + P], words, ident[:])
+
+        for q in range(4):
+            turn_back(q, 0)
+
+        w2_bf = tile("w2_bf", [P, N * 4], BF16, tag="last")
+        nc.vector.tensor_copy(
+            w2_bf[:].rearrange("p (c i u e) -> p c u e i", i=4, u=2, e=2),
+            raw_w2[:].rearrange("p (e u) (c i) -> p c u e i", u=2, i=4),
+        )
+        w2_codes = tile("w2_codes", [P, N], U32)
+        w2_scales = tile("w2_scales", [P, N], U8)
+        nc.vector.quantize_mx(w2_codes[:].bitcast(FP8X4), w2_scales[:], w2_bf[:])
+
+        for hf in range(2):
+            close_sum(3, hf, sums[3, hf])
+        round_sum(3, 0, sums[3, 0], nc.scalar.copy)
+        round_sum(3, 1, sums[3, 1], nc.vector.tensor_copy)
+
+        zq = [tile(f"zq{q}", [P, QUARTER * 4], BF16) for q in range(4)]
+        for q in range(4):
+            turn_back(q, 1)
+            copy = nc.vector.tensor_copy if q == 1 else nc.scalar.copy
+            copy(zq[q][:].bitcast(F32).rearrange("p (v u) -> p v u", u=2), back[q][:].rearrange("p (u v) -> p v u", u=2))
+        for q in range(4):
+            z_codes = tile(f"z_codes{q}", [P, QUARTER], U32)
+            z_scales = tile(f"z_scales{q}", [P, QUARTER], U8)
+            nc.vector.quantize_mx(z_codes[:].bitcast(FP8X4), z_scales[:], zq[q][:])
+            res = bank(f"res{q}", ("C0", "C1", "A0", "A1")[q])
+            nc.tensor.matmul_mx(res[:, :QUARTER], lhsT=w2_codes[:].bitcast(FP8X4), lhsT_scale=w2_scales[:],
+                                rhs=z_codes[:].bitcast(FP8X4), rhs_scale=z_scales[:], start=True, stop=True)
+            res_sb = tile(f"res_sb{q}", [P, QUARTER], F32)
+            nc.scalar.copy(res_sb[:], res[:, :QUARTER])
+            nc.sync.dma_start(out[:, q * QUARTER : (q + 1) * QUARTER], res_sb[:])

@@ -13,6 +13,7 @@ U32 = mybir.dt.uint32
 U16 = mybir.dt.uint16
 U8 = mybir.dt.uint8
 FP8X4 = mybir.dt.float8_e4m3fn_x4
+ADD = mybir.AluOpType.add
 
 P = 128
 PASSES = 2
@@ -46,12 +47,23 @@ def tile_picked_unet_none_p_kernel(tc, x_words, x_scales, w1, w2, skip, offs, ce
             nc.sync.dma_start(xs[32 * q : 32 * q + 8, :].bitcast(I32), xs_dram[:, 4 * q : 4 * q + 4, :])
 
         w1_rows = w1.rearrange("(g p j) c -> g p j c", g=PASSES, j=4)
-        raw0 = tile("raw0", [P, PASSES, 4, P], F32)
+        raw_lo = tile("raw_lo", [P, PASSES, 4, 2 * P], F32)
         for g in range(PASSES):
-            nc.sync.dma_start(raw0[:, g], w1_rows[g, :, :, 0:P])
+            nc.sync.dma_start(raw_lo[:, g], w1_rows[g, :, :, : 2 * P])
         xw = [tile(f"xw{g}", [P, T], U32) for g in range(PASSES)]
         for g in range(PASSES):
             nc.sync.dma_start(xw[g][:].bitcast(I32), x_words[g].rearrange("p n t -> p (n t)").bitcast(I32))
+        raw_hi = [tile(f"raw_hi{g}", [P, 4, 2 * P], F32) for g in range(PASSES)]
+        for g in range(PASSES):
+            nc.sync.dma_start(raw_hi[g][:], w1_rows[g, :, :, 2 * P :])
+        skip_rows = skip.rearrange("(p t) v -> p t v", t=4)
+        skip01 = [tile(f"skip{w}", [P, U], F32) for w in range(2)]
+        for w in range(2):
+            nc.sync.dma_start(skip01[w][:], skip_rows[64 * w : 64 * (w + 1), 0:2, :])
+        skip23 = tile("skip23", [P, 2, U], F32)
+        nc.sync.dma_start(skip23[:], skip_rows[:, 2:4, :])
+        raw_w2 = tile("raw_w2", [P, 4, N], F32)
+        nc.sync.dma_start(raw_w2[:], w2.rearrange("(p j) n -> p j n", j=4))
 
         ident = tile("ident", [P, P], F32)
         make_identity(nc, ident[:])
@@ -64,52 +76,42 @@ def tile_picked_unet_none_p_kernel(tc, x_words, x_scales, w1, w2, skip, offs, ce
 
         w1_codes, w1_scales = {}, {}
 
-        def quantize_w1_single(w, raw):
-            grouped = tile(f"w1_bf{w}", [P, PASSES * P * 4], BF16)
-            nc.scalar.copy(
-                grouped[:].rearrange("p (g c i j) -> p g c j i", g=PASSES, i=4, j=4),
-                raw[:].rearrange("p g j (c i) -> p g c j i", i=4),
-            )
-            codes = tile(f"w1_codes{w}", [P, PASSES * P], U32)
-            scales = tile(f"w1_scales{w}", [P, PASSES * P], U8)
-            nc.vector.quantize_mx(codes[:].bitcast(FP8X4), scales[:], grouped[:])
-            for g in range(PASSES):
-                w1_codes[w, g] = codes[:, g * P : (g + 1) * P]
-                w1_scales[w, g] = scales[:, g * P : (g + 1) * P]
+        def quantize_w1(name, grouped, windows):
+            width = len(windows) * PASSES * P
+            codes = tile(f"w1_codes{name}", [P, width], U32)
+            scales = tile(f"w1_scales{name}", [P, width], U8)
+            nc.vector.quantize_mx(codes[:].bitcast(FP8X4), scales[:], grouped)
+            for n, w in enumerate(windows):
+                for g in range(PASSES):
+                    at = (n * PASSES + g) * P
+                    w1_codes[w, g] = codes[:, at : at + P]
+                    w1_scales[w, g] = scales[:, at : at + P]
 
-        quantize_w1_single(0, raw0)
-        raw1 = tile("raw1", [P, PASSES, 4, P], F32, tag="raw0")
-        for g in range(PASSES):
-            nc.sync.dma_start(raw1[:, g], w1_rows[g, :, :, P : 2 * P])
+        bf0 = tile("w1_bf0", [P, PASSES, 64, 2, 4], BF16)
+        bf1 = tile("w1_bf1", [P, PASSES, 64, 2, 4], BF16)
+        bf23 = tile("w1_bf23", [P, 2, PASSES, P, 4], BF16)
+        lo = raw_lo[:].rearrange("p g j (m t) -> p g m j t", t=4)
+        nc.scalar.copy(bf0[:].rearrange("p g m e j -> p g m j e"), lo[:, :, :, :, 0:2])
+        quantize_w1("0", bf0[:].rearrange("p g m e j -> p (g m e j)"), [0])
+        nc.scalar.copy(bf23[:, :, :, :64, :].rearrange("p u g m j -> p g m j u"), lo[:, :, :, :, 2:4])
 
         gw = [tile(f"gw{g}", [P, S], U32) for g in range(PASSES)]
         nc.vector.tensor_copy(gw[0][:], xw[0][:].indirect(offs_t[:]))
         for a in (0, S // 2):
             nc.vector.tensor_copy(gw[1][:, a : a + S // 2], xw[1][:].indirect(offs_t[:, a // 16 : (a + S // 2) // 16]))
 
-        raw23 = [tile(f"raw23_{g}", [P, 4, 2 * P], F32, tag=("w1_bf0", "xw0")[g]) for g in range(PASSES)]
-        for g in range(PASSES):
-            nc.sync.dma_start(raw23[g][:], w1_rows[g, :, :, 2 * P : 4 * P])
-        skip01 = tile("skip01", [P, 2, U], F32, tag="xw1")
-        for w in range(2):
-            nc.sync.dma_start(skip01[:, w, :], skip[w * P : (w + 1) * P, :])
-
-        def h_pass(acc, w, g, a, b, at):
-            nc.tensor.matmul_mx(
-                acc[:, at : at + b - a],
-                lhsT=w1_codes[w, g].bitcast(FP8X4),
-                lhsT_scale=w1_scales[w, g],
-                rhs=gw[g][:, a:b].bitcast(FP8X4),
-                rhs_scale=gs[4 * g :, a:b],
-                start=(g == 0),
-                stop=(g == PASSES - 1),
-            )
-
         def h_product(w, a, b, tag):
             acc = bank(f"h{w}_{a}", tag)
-            for lo in range(a, b, QUARTER):
-                for g in range(PASSES):
-                    h_pass(acc, w, g, lo, min(lo + QUARTER, b), lo - a)
+            for g in range(PASSES):
+                nc.tensor.matmul_mx(
+                    acc[:, : b - a],
+                    lhsT=w1_codes[w, g].bitcast(FP8X4),
+                    lhsT_scale=w1_scales[w, g],
+                    rhs=gw[g][:, a:b].bitcast(FP8X4),
+                    rhs_scale=gs[4 * g :, a:b],
+                    start=(g == 0),
+                    stop=(g == PASSES - 1),
+                )
             return acc
 
         def h_scatter(w, a, b, acc, tag=None, copy=nc.scalar.copy):
@@ -118,121 +120,79 @@ def tile_picked_unet_none_p_kernel(tc, x_words, x_scales, w1, w2, skip, offs, ce
             nc.vector.tensor_copy(win[w][:].indirect(cell_t[:, a // 16 : b // 16]), stage[:])
 
         half = S // 2
-        acc00 = h_product(0, 0, half, "B0")
+        first = 128
+        acc00 = h_product(0, 0, first, "B0")
+        acc0m = h_product(0, first, half, "B2")
         acc01 = h_product(0, half, S, "B1")
-        h_scatter(0, 0, half, acc00, copy=nc.vector.tensor_copy)
-        quantize_w1_single(1, raw1)
-        h_scatter(0, half, S, acc01, tag="raw0")
-        skip23 = tile("skip23", [P, 2, U], F32, tag="w1_bf1")
-        nc.sync.dma_start(skip23[:], skip[2 * P :, :].rearrange("(p u) v -> p u v", u=2))
-        skips = [skip01[:, 0, :], skip01[:, 1, :], skip23[:, 0, :], skip23[:, 1, :]]
-
-        acc10 = h_product(1, 0, half, "B2")
-        acc11 = h_product(1, half, S, "B3")
-        h_scatter(1, 0, half, acc10)
-        grouped23 = tile("w1_bf23", [P, 2, PASSES, P * 4], BF16)
+        h_scatter(0, 0, first, acc00, copy=nc.vector.tensor_copy)
+        h_scatter(0, first, half, acc0m, copy=nc.vector.tensor_copy)
         for g in range(PASSES):
-            nc.scalar.copy(
-                grouped23[:, :, g, :].rearrange("p u (c i j) -> p c j i u", i=2, j=4),
-                raw23[g][:].rearrange("p j (c i u) -> p c j i u", i=2, u=2),
-            )
-        codes23 = tile("w1_codes23", [P, 2 * PASSES * P], U32)
-        scales23 = tile("w1_scales23", [P, 2 * PASSES * P], U8)
-        nc.vector.quantize_mx(codes23[:].bitcast(FP8X4), scales23[:], grouped23[:].rearrange("p u g x -> p (u g x)"))
-        for u in range(2):
-            for g in range(PASSES):
-                at = (u * PASSES + g) * P
-                w1_codes[2 + u, g] = codes23[:, at : at + P]
-                w1_scales[2 + u, g] = scales23[:, at : at + P]
-        h_scatter(1, half, S, acc11, tag="xw0")
-        raw_w2 = tile("raw_w2", [P, 4, N], F32, tag="w1_bf23")
-        nc.sync.dma_start(raw_w2[:], w2.rearrange("(p j) n -> p j n", j=4))
+            hi = raw_hi[g][:].rearrange("p j (m t) -> p m j t", t=4)
+            nc.scalar.copy(bf1[:, g].rearrange("p m e j -> p m j e"), hi[:, :, :, 0:2])
+            nc.scalar.copy(bf23[:, :, g, 64:, :].rearrange("p u m j -> p m j u"), hi[:, :, :, 2:4])
+        quantize_w1("1", bf1[:].rearrange("p g m e j -> p (g m e j)"), [1])
+        quantize_w1("23", bf23[:].rearrange("p u g m j -> p (u g m j)"), [2, 3])
+        h_scatter(0, half, S, acc01, tag="raw_hi1")
 
-        cut = 384
-        acc20 = h_product(2, 0, half, "B0")
-        acc21 = h_product(2, half, S, "B1")
-        acc30 = h_product(3, 0, cut, "B2")
-        h_scatter(2, 0, half, acc20)
-        h_scatter(2, half, S, acc21)
-        h_scatter(3, 0, cut, acc30)
+        pieces = [(1, 0, half, "B2"), (1, half, S, "B3"), (2, 0, S, "B0")]
+        for w, a, b, tag in pieces:
+            h_scatter(w, a, b, h_product(w, a, b, tag))
+        acc3 = h_product(3, 0, S, "B1")
+        stage3 = tile("h_sb3", [P, S], F32)
+        nc.scalar.copy(stage3[:], acc3[:])
 
-        zt = [tile(f"zt{hf}", [P, 2, 4, 2 * P], BF16) for hf in range(2)]
-
-        def open_sum(w, hf, tag):
-            acc = bank(f"z{w}_{hf}", tag)
-            for c in range(4):
-                cols = slice((4 * hf + c) * P, (4 * hf + c + 1) * P)
-                nc.tensor.matmul(acc[:, c * P : (c + 1) * P], lhsT=skips[w][:, cols], rhs=ident[:],
-                                 is_transpose=True, start=(c == 0), stop=False)
-            return acc
-
-        def close_sum(w, hf, acc):
-            for c in range(4):
-                cols = slice((4 * hf + c) * P, (4 * hf + c + 1) * P)
-                nc.tensor.matmul(acc[:, c * P : (c + 1) * P], lhsT=win[w][:, cols], rhs=ident[:],
-                                 is_transpose=True, start=False, stop=(c == 3))
-
-        def round_sum(w, hf, acc, copy):
-            if w < 2:
-                copy(zt[hf][:, :, :, 64 * w : 64 * (w + 1)], acc[:].rearrange("p (c x u) -> p u c x", c=4, u=2))
-            else:
-                copy(zt[hf][:, w - 2, :, P:], acc[:].rearrange("p (c x) -> p c x", c=4))
-
-        sums = {}
+        zt = [tile(f"zt{hf}", [P, 4, 2 * P], BF16) for hf in range(2)]
         for w, tag in ((0, "A"), (1, "C")):
+            sums = [bank(f"z{w}_{hf}", f"{tag}{hf}") for hf in range(2)]
+            for source, opening in ((skip01[w], True), (win[w], False)):
+                for c in range(8):
+                    nc.tensor.matmul(sums[c // 4][:, (c % 4) * P : (c % 4 + 1) * P], lhsT=source[:, c * P : (c + 1) * P],
+                                     rhs=ident[:], is_transpose=True,
+                                     start=(opening and c % 4 == 0), stop=(not opening and c % 4 == 3))
             for hf in range(2):
-                sums[w, hf] = open_sum(w, hf, f"{tag}{hf}")
-            for hf in range(2):
-                close_sum(w, hf, sums[w, hf])
-                round_sum(w, hf, sums[w, hf], nc.scalar.copy)
+                nc.scalar.copy(zt[hf][:, :, w * P : (w + 1) * P], sums[hf][:].rearrange("p (c x) -> p c x", c=4))
+
+        pairs = [tile(f"pairs{q}", [P, 2, QUARTER, 2], BF16) for q in range(4)]
         for hf in range(2):
-            sums[3, hf] = open_sum(3, hf, f"A{hf}")
-        for hf in range(2):
-            sums[2, hf] = open_sum(2, hf, f"C{hf}")
-        for hf in range(2):
-            close_sum(2, hf, sums[2, hf])
-            round_sum(2, hf, sums[2, hf], nc.scalar.copy)
-
-        acc31 = h_product(3, cut, S, "C0")
-        h_scatter(3, cut, S, acc31, tag="last")
-
-        back = [bank(f"back{q}", f"B{q}") for q in range(4)]
-
-        def turn_back(q, u):
-            for c in range(2):
-                words = zt[q // 2][:, u, 2 * (q % 2) + c, :].bitcast(F32)
-                at = u * QUARTER + c * P
-                nc.tensor.transpose(back[q][:, at : at + P], words, ident[:])
-
+            back = bank(f"back{hf}", f"A{hf}")
+            for c in range(4):
+                nc.tensor.transpose(back[:, c * P : (c + 1) * P], zt[hf][:, c, :].bitcast(F32), ident[:])
+            for q in (2 * hf, 2 * hf + 1):
+                nc.scalar.copy(pairs[q][:, 0].rearrange("p v e -> p (v e)").bitcast(F32),
+                               back[:, (q % 2) * QUARTER : (q % 2 + 1) * QUARTER])
+        z2 = tile("z2", [P, U], BF16, tag="zt0")
+        nc.vector.scalar_tensor_tensor(z2[:], win[2][:], win[3][:, 0:1], skip23[:, 0, :], ADD, ADD)
+        nc.vector.tensor_copy(win[3][:].indirect(cell_t[:]), stage3[:])
         for q in range(4):
-            turn_back(q, 0)
+            cols = slice(q * QUARTER, (q + 1) * QUARTER)
+            nc.scalar.copy(pairs[q][:, 1], z2[:, cols].unsqueeze(2).to_broadcast([P, QUARTER, 2]))
 
-        w2_bf = tile("w2_bf", [P, N * 4], BF16, tag="last")
-        nc.vector.tensor_copy(
-            w2_bf[:].rearrange("p (c i u e) -> p c u e i", i=4, u=2, e=2),
-            raw_w2[:].rearrange("p (e u) (c i) -> p c u e i", u=2, i=4),
+        w2_bf = tile("w2_bf", [P, N * 4], BF16)
+        nc.scalar.copy(
+            w2_bf[:].rearrange("p (c i j) -> p c j i", i=4, j=4),
+            raw_w2[:].rearrange("p j (c i) -> p c j i", i=4),
         )
         w2_codes = tile("w2_codes", [P, N], U32)
         w2_scales = tile("w2_scales", [P, N], U8)
         nc.vector.quantize_mx(w2_codes[:].bitcast(FP8X4), w2_scales[:], w2_bf[:])
 
-        for hf in range(2):
-            close_sum(3, hf, sums[3, hf])
-        round_sum(3, 0, sums[3, 0], nc.scalar.copy)
-        round_sum(3, 1, sums[3, 1], nc.vector.tensor_copy)
-
         zq = [tile(f"zq{q}", [P, QUARTER * 4], BF16) for q in range(4)]
         for q in range(4):
-            turn_back(q, 1)
-            copy = nc.vector.tensor_copy if q == 1 else nc.scalar.copy
-            copy(zq[q][:].bitcast(F32).rearrange("p (v u) -> p v u", u=2), back[q][:].rearrange("p (u v) -> p v u", u=2))
+            cols = slice(q * QUARTER, (q + 1) * QUARTER)
+            nc.vector.tensor_tensor(pairs[q][:, 1, :, 1], win[3][:, cols], skip23[:, 1, cols], ADD)
         for q in range(4):
-            z_codes = tile(f"z_codes{q}", [P, QUARTER], U32)
-            z_scales = tile(f"z_scales{q}", [P, QUARTER], U8)
-            nc.vector.quantize_mx(z_codes[:].bitcast(FP8X4), z_scales[:], zq[q][:])
-            res = bank(f"res{q}", ("C0", "C1", "A0", "A1")[q])
-            nc.tensor.matmul_mx(res[:, :QUARTER], lhsT=w2_codes[:].bitcast(FP8X4), lhsT_scale=w2_scales[:],
+            words = pairs[q][:].rearrange("p u v e -> p (u v e)").bitcast(F32)
+            nc.scalar.copy(zq[q][:].bitcast(F32).rearrange("p (v u) -> p v u", u=2), words.rearrange("p (u v) -> p v u", u=2))
+        pieces_out = [(0, 256), (256, 512), (512, 768), (768, 896), (896, 1024)]
+        for n, (a, b) in enumerate(pieces_out):
+            q, at, width = a // QUARTER, a % QUARTER, b - a
+            z_codes = tile(f"z_codes{n}", [P, width], U32)
+            z_scales = tile(f"z_scales{n}", [P, width], U8)
+            nc.vector.quantize_mx(z_codes[:].bitcast(FP8X4), z_scales[:], zq[q][:, 4 * at : 4 * (at + width)])
+            res = bank(f"res{n}", ("B0", "B1", "B2", "B3", "C0")[n])
+            nc.tensor.matmul_mx(res[:, :width], lhsT=w2_codes[:].bitcast(FP8X4), lhsT_scale=w2_scales[:],
                                 rhs=z_codes[:].bitcast(FP8X4), rhs_scale=z_scales[:], start=True, stop=True)
-            res_sb = tile(f"res_sb{q}", [P, QUARTER], F32)
-            nc.scalar.copy(res_sb[:], res[:, :QUARTER])
-            nc.sync.dma_start(out[:, q * QUARTER : (q + 1) * QUARTER], res_sb[:])
+            res_sb = tile(f"res_sb{n}", [P, width], F32)
+            copy = nc.vector.tensor_copy if n == len(pieces_out) - 1 else nc.scalar.copy
+            copy(res_sb[:], res[:, :width])
+            nc.sync.dma_start(out[:, a:b], res_sb[:])

@@ -36,9 +36,11 @@ def tile_picked_unet_none_p_kernel(tc, x_words, x_scales, w1, w2, skip, offs, ce
 
         offs_t = sb.tile([P, S // 16], U16, name="offs_t")
         nc.sync.dma_start(offs_t[:], offs)
-        cell_t = sb.tile([P, S // 16], U16, name="cell_t")
-        nc.sync.dma_start(cell_t[:], cell)
 
+        w1_rows = w1.rearrange("(g p j) c -> g p j c", g=PASSES, j=4)
+        raw_lo = tile("raw_lo", [P, PASSES, 4, 2 * P], F32)
+        for g in range(PASSES):
+            nc.sync.dma_start(raw_lo[:, g], w1_rows[g, :, :, : 2 * P])
         xs = tile("xs", [P, T], U8)
         nc.gpsimd.memset(xs[:, : T // 2].bitcast(I32), 0)
         nc.vector.memset(xs[:, T // 2 :].bitcast(I32), 0)
@@ -46,13 +48,11 @@ def tile_picked_unet_none_p_kernel(tc, x_words, x_scales, w1, w2, skip, offs, ce
         for q in range(4):
             nc.sync.dma_start(xs[32 * q : 32 * q + 8, :].bitcast(I32), xs_dram[:, 4 * q : 4 * q + 4, :])
 
-        w1_rows = w1.rearrange("(g p j) c -> g p j c", g=PASSES, j=4)
-        raw_lo = tile("raw_lo", [P, PASSES, 4, 2 * P], F32)
-        for g in range(PASSES):
-            nc.sync.dma_start(raw_lo[:, g], w1_rows[g, :, :, : 2 * P])
         xw = [tile(f"xw{g}", [P, T], U32) for g in range(PASSES)]
         for g in range(PASSES):
             nc.sync.dma_start(xw[g][:].bitcast(I32), x_words[g].rearrange("p n t -> p (n t)").bitcast(I32))
+        cell_t = sb.tile([P, S // 16], U16, name="cell_t")
+        nc.sync.dma_start(cell_t[:], cell)
         raw_hi = [tile(f"raw_hi{g}", [P, 4, 2 * P], F32) for g in range(PASSES)]
         for g in range(PASSES):
             nc.sync.dma_start(raw_hi[g][:], w1_rows[g, :, :, 2 * P :])
@@ -72,7 +72,8 @@ def tile_picked_unet_none_p_kernel(tc, x_words, x_scales, w1, w2, skip, offs, ce
             (nc.vector if w < 2 else nc.gpsimd).memset(win[w][:], 0.0)
 
         gs = tile("gs", [P, S], U8)
-        nc.vector.tensor_copy(gs[:], xs[:].indirect(offs_t[:]))
+        for a in (0, S // 2):
+            nc.vector.tensor_copy(gs[:, a : a + S // 2], xs[:].indirect(offs_t[:, a // 16 : (a + S // 2) // 16]))
 
         w1_codes, w1_scales = {}, {}
 
@@ -94,6 +95,19 @@ def tile_picked_unet_none_p_kernel(tc, x_words, x_scales, w1, w2, skip, offs, ce
         nc.scalar.copy(bf0[:].rearrange("p g m e j -> p g m j e"), lo[:, :, :, :, 0:2])
         quantize_w1("0", bf0[:].rearrange("p g m e j -> p (g m e j)"), [0])
         nc.scalar.copy(bf23[:, :, :, :64, :].rearrange("p u g m j -> p g m j u"), lo[:, :, :, :, 2:4])
+        codes23 = tile("w1_codes23", [P, 2, PASSES, P], U32)
+        scales23 = tile("w1_scales23", [P, 2, PASSES, P], U8)
+
+        def quantize_half23(part):
+            cols = slice(64 * part, 64 * (part + 1))
+            for u in range(2):
+                for g in range(PASSES):
+                    nc.vector.quantize_mx(codes23[:, u, g, cols].bitcast(FP8X4), scales23[:, u, g, cols],
+                                          bf23[:, u, g, cols, :].rearrange("p m j -> p (m j)"))
+                    w1_codes[2 + u, g] = codes23[:, u, g, :]
+                    w1_scales[2 + u, g] = scales23[:, u, g, :]
+
+        quantize_half23(0)
 
         gw = [tile(f"gw{g}", [P, S], U32) for g in range(PASSES)]
         nc.vector.tensor_copy(gw[0][:], xw[0][:].indirect(offs_t[:]))
@@ -131,7 +145,7 @@ def tile_picked_unet_none_p_kernel(tc, x_words, x_scales, w1, w2, skip, offs, ce
             nc.scalar.copy(bf1[:, g].rearrange("p m e j -> p m j e"), hi[:, :, :, 0:2])
             nc.scalar.copy(bf23[:, :, g, 64:, :].rearrange("p u m j -> p m j u"), hi[:, :, :, 2:4])
         quantize_w1("1", bf1[:].rearrange("p g m e j -> p (g m e j)"), [1])
-        quantize_w1("23", bf23[:].rearrange("p u g m j -> p (u g m j)"), [2, 3])
+        quantize_half23(1)
         h_scatter(0, half, S, acc01, tag="raw_hi1")
 
         pieces = [(1, 0, half, "B2"), (1, half, S, "B3"), (2, 0, S, "B0")]
@@ -161,10 +175,10 @@ def tile_picked_unet_none_p_kernel(tc, x_words, x_scales, w1, w2, skip, offs, ce
                 nc.scalar.copy(pairs[q][:, 0].rearrange("p v e -> p (v e)").bitcast(F32),
                                back[:, (q % 2) * QUARTER : (q % 2 + 1) * QUARTER])
         z2 = tile("z2", [P, U], BF16, tag="zt0")
-        nc.vector.scalar_tensor_tensor(z2[:], win[2][:], win[3][:, 0:1], skip23[:, 0, :], ADD, ADD)
         nc.vector.tensor_copy(win[3][:].indirect(cell_t[:]), stage3[:])
         for q in range(4):
             cols = slice(q * QUARTER, (q + 1) * QUARTER)
+            nc.gpsimd.tensor_tensor(z2[:, cols], win[2][:, cols], skip23[:, 0, cols], ADD)
             nc.scalar.copy(pairs[q][:, 1], z2[:, cols].unsqueeze(2).to_broadcast([P, QUARTER, 2]))
 
         w2_bf = tile("w2_bf", [P, N * 4], BF16)

@@ -58,10 +58,10 @@ def tile_picked_unet_none_p_kernel(tc, x_words, x_scales, w1, w2, skip, offs, ce
             nc.sync.dma_start(raw_hi[g][:], w1_rows[g, :, :, 2 * P :])
         skip_rows = skip.rearrange("(p t) v -> p t v", t=4)
         skip01 = [tile(f"skip{w}", [P, U], F32) for w in range(2)]
-        for w in range(2):
-            nc.sync.dma_start(skip01[w][:], skip_rows[64 * w : 64 * (w + 1), 0:2, :])
         skip23 = tile("skip23", [P, 2, U], F32)
+        nc.sync.dma_start(skip01[0][:], skip_rows[:64, 0:2, :])
         nc.sync.dma_start(skip23[:], skip_rows[:, 2:4, :])
+        nc.sync.dma_start(skip01[1][:], skip_rows[64:, 0:2, :])
         raw_w2 = tile("raw_w2", [P, 4, N], F32)
         nc.sync.dma_start(raw_w2[:], w2.rearrange("(p j) n -> p j n", j=4))
 
@@ -139,7 +139,7 @@ def tile_picked_unet_none_p_kernel(tc, x_words, x_scales, w1, w2, skip, offs, ce
         acc0m = h_product(0, first, half, "B2")
         acc01 = h_product(0, half, S, "B1")
         h_scatter(0, 0, first, acc00, copy=nc.vector.tensor_copy)
-        h_scatter(0, first, half, acc0m, copy=nc.vector.tensor_copy)
+        h_scatter(0, first, half, acc0m)
         for g in range(PASSES):
             hi = raw_hi[g][:].rearrange("p j (m t) -> p m j t", t=4)
             nc.scalar.copy(bf1[:, g].rearrange("p m e j -> p m j e"), hi[:, :, :, 0:2])
@@ -148,12 +148,19 @@ def tile_picked_unet_none_p_kernel(tc, x_words, x_scales, w1, w2, skip, offs, ce
         quantize_half23(1)
         h_scatter(0, half, S, acc01, tag="raw_hi1")
 
-        pieces = [(1, 0, half, "B2"), (1, half, S, "B3"), (2, 0, S, "B0")]
+        pieces = [(2, 0, half, "B2"), (2, half, S, "B3"), (1, 0, S, "B2")]
         for w, a, b, tag in pieces:
             h_scatter(w, a, b, h_product(w, a, b, tag))
-        acc3 = h_product(3, 0, S, "B1")
+        acc3 = h_product(3, 0, S, "B3")
         stage3 = tile("h_sb3", [P, S], F32)
         nc.scalar.copy(stage3[:], acc3[:])
+
+        pairs = [tile(f"pairs{q}", [P, 2, QUARTER, 2], BF16) for q in range(4)]
+        for q in range(4):
+            cols = slice(q * QUARTER, (q + 1) * QUARTER)
+            z2 = tile(f"z2_{q}", [P, QUARTER], BF16)
+            nc.gpsimd.tensor_tensor(z2[:], win[2][:, cols], skip23[:, 0, cols], ADD)
+            nc.scalar.copy(pairs[q][:, 1], z2[:].unsqueeze(2).to_broadcast([P, QUARTER, 2]))
 
         zt = [tile(f"zt{hf}", [P, 4, 2 * P], BF16) for hf in range(2)]
         for w, tag in ((0, "A"), (1, "C")):
@@ -166,7 +173,6 @@ def tile_picked_unet_none_p_kernel(tc, x_words, x_scales, w1, w2, skip, offs, ce
             for hf in range(2):
                 nc.scalar.copy(zt[hf][:, :, w * P : (w + 1) * P], sums[hf][:].rearrange("p (c x) -> p c x", c=4))
 
-        pairs = [tile(f"pairs{q}", [P, 2, QUARTER, 2], BF16) for q in range(4)]
         for hf in range(2):
             back = bank(f"back{hf}", f"A{hf}")
             for c in range(4):
@@ -174,12 +180,7 @@ def tile_picked_unet_none_p_kernel(tc, x_words, x_scales, w1, w2, skip, offs, ce
             for q in (2 * hf, 2 * hf + 1):
                 nc.scalar.copy(pairs[q][:, 0].rearrange("p v e -> p (v e)").bitcast(F32),
                                back[:, (q % 2) * QUARTER : (q % 2 + 1) * QUARTER])
-        z2 = tile("z2", [P, U], BF16, tag="zt0")
         nc.vector.tensor_copy(win[3][:].indirect(cell_t[:]), stage3[:])
-        for q in range(4):
-            cols = slice(q * QUARTER, (q + 1) * QUARTER)
-            nc.gpsimd.tensor_tensor(z2[:, cols], win[2][:, cols], skip23[:, 0, cols], ADD)
-            nc.scalar.copy(pairs[q][:, 1], z2[:, cols].unsqueeze(2).to_broadcast([P, QUARTER, 2]))
 
         w2_bf = tile("w2_bf", [P, N * 4], BF16)
         nc.scalar.copy(

@@ -37,33 +37,36 @@ def tile_picked_unet_none_p_kernel(tc, x_words, x_scales, w1, w2, skip, offs, ce
         offs_t = sb.tile([P, S // 16], U16, name="offs_t")
         nc.sync.dma_start(offs_t[:], offs)
 
+        xw = [tile(f"xw{g}", [P, T], U32) for g in range(PASSES)]
         w1_rows = w1.rearrange("(g p j) c -> g p j c", g=PASSES, j=4)
-        raw_lo = tile("raw_lo", [P, PASSES, 4, 2 * P], F32)
-        for g in range(PASSES):
-            nc.sync.dma_start(raw_lo[:, g], w1_rows[g, :, :, : 2 * P])
+        raw_lo = [tile(f"raw_lo{g}", [P, 4, 2 * P], F32) for g in range(PASSES)]
+        raw_hi = [tile(f"raw_hi{g}", [P, 4, 2 * P], F32) for g in range(PASSES)]
         xs = tile("xs", [P, T], U8)
-        nc.gpsimd.memset(xs[:, : T // 2].bitcast(I32), 0)
-        nc.vector.memset(xs[:, T // 2 :].bitcast(I32), 0)
+        nc.vector.memset(xs[:].bitcast(I32), 0)
         xs_dram = x_scales.bitcast(I32)
+
+        def load_words(g):
+            nc.sync.dma_start(xw[g][:].bitcast(I32), x_words[g].rearrange("p n t -> p (n t)").bitcast(I32))
+
+        load_words(0)
+        nc.sync.dma_start(raw_lo[0][:], w1_rows[0, :, :, : 2 * P])
         for q in range(4):
             nc.sync.dma_start(xs[32 * q : 32 * q + 8, :].bitcast(I32), xs_dram[:, 4 * q : 4 * q + 4, :])
-
-        xw = [tile(f"xw{g}", [P, T], U32) for g in range(PASSES)]
-        for g in range(PASSES):
-            nc.sync.dma_start(xw[g][:].bitcast(I32), x_words[g].rearrange("p n t -> p (n t)").bitcast(I32))
+        load_words(1)
+        nc.sync.dma_start(raw_lo[1][:], w1_rows[1, :, :, : 2 * P])
         cell_t = sb.tile([P, S // 16], U16, name="cell_t")
         nc.sync.dma_start(cell_t[:], cell)
-        raw_hi = [tile(f"raw_hi{g}", [P, 4, 2 * P], F32) for g in range(PASSES)]
         for g in range(PASSES):
             nc.sync.dma_start(raw_hi[g][:], w1_rows[g, :, :, 2 * P :])
-        skip_rows = skip.rearrange("(p t) v -> p t v", t=4)
-        skip01 = [tile(f"skip{w}", [P, U], F32) for w in range(2)]
-        skip23 = tile("skip23", [P, 2, U], F32)
-        nc.sync.dma_start(skip01[0][:], skip_rows[:64, 0:2, :])
-        nc.sync.dma_start(skip23[:], skip_rows[:, 2:4, :])
-        nc.sync.dma_start(skip01[1][:], skip_rows[64:, 0:2, :])
         raw_w2 = tile("raw_w2", [P, 4, N], F32)
         nc.sync.dma_start(raw_w2[:], w2.rearrange("(p j) n -> p j n", j=4))
+        skip_rows = skip.rearrange("(p t) v -> p t v", t=4)
+        skip_sb = {w: tile(f"skip{w}", [P, U], F32) for w in (0, 1, 3)}
+        words = tile("words", [P, 4, 2, QUARTER], F32)
+        nc.sync.dma_start(skip_sb[0][:], skip_rows[:64, 0:2, :])
+        nc.sync.dma_start(skip_sb[1][:], skip_rows[64:, 0:2, :])
+        nc.sync.dma_start(words[:, :, 1, :], skip_rows[:, 2, :].rearrange("p (q v) -> p q v", q=4))
+        nc.sync.dma_start(skip_sb[3][:], skip_rows[:, 3, :])
 
         ident = tile("ident", [P, P], F32)
         make_identity(nc, ident[:])
@@ -72,116 +75,76 @@ def tile_picked_unet_none_p_kernel(tc, x_words, x_scales, w1, w2, skip, offs, ce
             (nc.vector if w < 2 else nc.gpsimd).memset(win[w][:], 0.0)
 
         gs = tile("gs", [P, S], U8)
-        for a in (0, S // 2):
-            nc.vector.tensor_copy(gs[:, a : a + S // 2], xs[:].indirect(offs_t[:, a // 16 : (a + S // 2) // 16]))
-
-        w1_codes, w1_scales = {}, {}
-
-        def quantize_w1(name, grouped, windows):
-            width = len(windows) * PASSES * P
-            codes = tile(f"w1_codes{name}", [P, width], U32)
-            scales = tile(f"w1_scales{name}", [P, width], U8)
-            nc.vector.quantize_mx(codes[:].bitcast(FP8X4), scales[:], grouped)
-            for n, w in enumerate(windows):
-                for g in range(PASSES):
-                    at = (n * PASSES + g) * P
-                    w1_codes[w, g] = codes[:, at : at + P]
-                    w1_scales[w, g] = scales[:, at : at + P]
-
-        bf0 = tile("w1_bf0", [P, PASSES, 64, 2, 4], BF16)
-        bf1 = tile("w1_bf1", [P, PASSES, 64, 2, 4], BF16)
-        bf23 = tile("w1_bf23", [P, 2, PASSES, P, 4], BF16)
-        lo = raw_lo[:].rearrange("p g j (m t) -> p g m j t", t=4)
-        nc.scalar.copy(bf0[:].rearrange("p g m e j -> p g m j e"), lo[:, :, :, :, 0:2])
-        quantize_w1("0", bf0[:].rearrange("p g m e j -> p (g m e j)"), [0])
-        nc.scalar.copy(bf23[:, :, :, :64, :].rearrange("p u g m j -> p g m j u"), lo[:, :, :, :, 2:4])
-        codes23 = tile("w1_codes23", [P, 2, PASSES, P], U32)
-        scales23 = tile("w1_scales23", [P, 2, PASSES, P], U8)
-
-        def quantize_half23(part):
-            cols = slice(64 * part, 64 * (part + 1))
-            for u in range(2):
-                for g in range(PASSES):
-                    nc.vector.quantize_mx(codes23[:, u, g, cols].bitcast(FP8X4), scales23[:, u, g, cols],
-                                          bf23[:, u, g, cols, :].rearrange("p m j -> p (m j)"))
-                    w1_codes[2 + u, g] = codes23[:, u, g, :]
-                    w1_scales[2 + u, g] = scales23[:, u, g, :]
-
-        quantize_half23(0)
-
+        nc.vector.tensor_copy(gs[:], xs[:].indirect(offs_t[:]))
         gw = [tile(f"gw{g}", [P, S], U32) for g in range(PASSES)]
-        nc.vector.tensor_copy(gw[0][:], xw[0][:].indirect(offs_t[:]))
-        for a in (0, S // 2):
-            nc.vector.tensor_copy(gw[1][:, a : a + S // 2], xw[1][:].indirect(offs_t[:, a // 16 : (a + S // 2) // 16]))
+        for g in range(PASSES):
+            nc.vector.tensor_copy(gw[g][:], xw[g][:].indirect(offs_t[:]))
 
-        def h_product(w, a, b, tag):
-            acc = bank(f"h{w}_{a}", tag)
+        bf23 = tile("w1_bf23", [P, 2, PASSES, P * 4], BF16)
+        bf = [tile(f"w1_bf{w}", [P, PASSES, P * 4], BF16)[:, :, :] for w in range(2)] + [bf23[:, u] for u in range(2)]
+        codes = [tile(f"w1_codes{w}", [P, PASSES, P], U32) for w in range(4)]
+        scales = [tile(f"w1_scales{w}", [P, PASSES, P], U8) for w in range(4)]
+
+        def raw_part(g, part):
+            return (raw_lo, raw_hi)[part][g][:].rearrange("p j (m t) -> p m j t", t=4)
+
+        def round_pairs(w, g, copy=nc.scalar.copy, a=0, b=64):
+            copy(bf[w][:, g].rearrange("p (m e j) -> p m j e", e=2, j=4)[:, a:b], raw_part(g, w)[:, a:b, :, 0:2])
+
+        def round_singles(g, part):
+            nc.scalar.copy(bf23[:, :, g].rearrange("p u (m j) -> p m j u", j=4)[:, 64 * part : 64 * (part + 1)],
+                           raw_part(g, part)[:, :, :, 2:4])
+            for w in (2, 3):
+                quantize_w1(w, g, 64 * part, 64 * (part + 1))
+
+        def quantize_w1(w, g, a, b):
+            nc.vector.quantize_mx(codes[w][:, g, a:b].bitcast(FP8X4), scales[w][:, g, a:b], bf[w][:, g, 4 * a : 4 * b])
+
+        def quantize_window(w):
+            nc.vector.quantize_mx(codes[w][:].rearrange("p g m -> p (g m)").bitcast(FP8X4),
+                                  scales[w][:].rearrange("p g m -> p (g m)"), bf[w].rearrange("p g x -> p (g x)"))
+
+        def h_product(acc, w, a, b):
             for g in range(PASSES):
                 nc.tensor.matmul_mx(
-                    acc[:, : b - a],
-                    lhsT=w1_codes[w, g].bitcast(FP8X4),
-                    lhsT_scale=w1_scales[w, g],
+                    acc,
+                    lhsT=codes[w][:, g].bitcast(FP8X4),
+                    lhsT_scale=scales[w][:, g],
                     rhs=gw[g][:, a:b].bitcast(FP8X4),
                     rhs_scale=gs[4 * g :, a:b],
                     start=(g == 0),
                     stop=(g == PASSES - 1),
                 )
-            return acc
 
-        def h_scatter(w, a, b, acc, tag=None, copy=nc.scalar.copy):
-            stage = tile(f"h_sb{w}_{a}", [P, b - a], F32, tag)
-            copy(stage[:], acc[:, : b - a])
-            nc.vector.tensor_copy(win[w][:].indirect(cell_t[:, a // 16 : b // 16]), stage[:])
+        def h_scatter(w, a, b, acc, copy=nc.scalar.copy, stage=None):
+            if stage is None:
+                stage = tile(f"h_sb{w}_{a}", [P, b - a], F32)[:, :]
+            copy(stage, acc)
+            nc.vector.tensor_copy(win[w][:].indirect(cell_t[:, a // 16 : b // 16]), stage)
 
         half = S // 2
         first = 128
-        acc00 = h_product(0, 0, first, "B0")
-        acc0m = h_product(0, first, half, "B2")
-        acc01 = h_product(0, half, S, "B1")
-        h_scatter(0, 0, first, acc00, copy=nc.vector.tensor_copy)
-        h_scatter(0, first, half, acc0m)
-        for g in range(PASSES):
-            hi = raw_hi[g][:].rearrange("p j (m t) -> p m j t", t=4)
-            nc.scalar.copy(bf1[:, g].rearrange("p m e j -> p m j e"), hi[:, :, :, 0:2])
-            nc.scalar.copy(bf23[:, :, g, 64:, :].rearrange("p u m j -> p m j u"), hi[:, :, :, 2:4])
-        quantize_w1("1", bf1[:].rearrange("p g m e j -> p (g m e j)"), [1])
-        quantize_half23(1)
-        h_scatter(0, half, S, acc01, tag="raw_hi1")
-
-        pieces = [(2, 0, half, "B2"), (2, half, S, "B3"), (1, 0, S, "B2")]
-        for w, a, b, tag in pieces:
-            h_scatter(w, a, b, h_product(w, a, b, tag))
-        acc3 = h_product(3, 0, S, "B3")
-        stage3 = tile("h_sb3", [P, S], F32)
-        nc.scalar.copy(stage3[:], acc3[:])
-
-        pairs = [tile(f"pairs{q}", [P, 2, QUARTER, 2], BF16) for q in range(4)]
-        for q in range(4):
-            cols = slice(q * QUARTER, (q + 1) * QUARTER)
-            z2 = tile(f"z2_{q}", [P, QUARTER], BF16)
-            nc.gpsimd.tensor_tensor(z2[:], win[2][:, cols], skip23[:, 0, cols], ADD)
-            nc.scalar.copy(pairs[q][:, 1], z2[:].unsqueeze(2).to_broadcast([P, QUARTER, 2]))
-
-        zt = [tile(f"zt{hf}", [P, 4, 2 * P], BF16) for hf in range(2)]
-        for w, tag in ((0, "A"), (1, "C")):
-            sums = [bank(f"z{w}_{hf}", f"{tag}{hf}") for hf in range(2)]
-            for source, opening in ((skip01[w], True), (win[w], False)):
-                for c in range(8):
-                    nc.tensor.matmul(sums[c // 4][:, (c % 4) * P : (c % 4 + 1) * P], lhsT=source[:, c * P : (c + 1) * P],
-                                     rhs=ident[:], is_transpose=True,
-                                     start=(opening and c % 4 == 0), stop=(not opening and c % 4 == 3))
-            for hf in range(2):
-                nc.scalar.copy(zt[hf][:, :, w * P : (w + 1) * P], sums[hf][:].rearrange("p (c x) -> p c x", c=4))
-
-        for hf in range(2):
-            back = bank(f"back{hf}", f"A{hf}")
-            for c in range(4):
-                nc.tensor.transpose(back[:, c * P : (c + 1) * P], zt[hf][:, c, :].bitcast(F32), ident[:])
-            for q in (2 * hf, 2 * hf + 1):
-                nc.scalar.copy(pairs[q][:, 0].rearrange("p v e -> p (v e)").bitcast(F32),
-                               back[:, (q % 2) * QUARTER : (q % 2 + 1) * QUARTER])
-        nc.vector.tensor_copy(win[3][:].indirect(cell_t[:]), stage3[:])
-
+        round_pairs(0, 0)
+        quantize_w1(0, 0, 0, P)
+        round_singles(0, 0)
+        round_pairs(0, 1, nc.vector.tensor_copy, 0, 40)
+        round_pairs(0, 1, nc.scalar.copy, 40, 64)
+        quantize_w1(0, 1, 0, P)
+        cuts = (0, first, S - first, S)
+        accs = []
+        for n in range(3):
+            acc = bank(f"h0_{n}", f"B{n}")[:, : cuts[n + 1] - cuts[n]]
+            h_product(acc, 0, cuts[n], cuts[n + 1])
+            accs.append(acc)
+        h_scatter(0, cuts[0], cuts[1], accs[0], copy=nc.vector.tensor_copy)
+        h_scatter(0, cuts[1], cuts[2], accs[1])
+        round_singles(1, 0)
+        round_singles(0, 1)
+        round_pairs(1, 0)
+        round_singles(1, 1)
+        round_pairs(1, 1)
+        quantize_window(1)
+        h_scatter(0, cuts[2], cuts[3], accs[2], stage=tile("h_sb0_last", [P, first], F32, "raw_hi1")[:, :])
         w2_bf = tile("w2_bf", [P, N * 4], BF16)
         nc.scalar.copy(
             w2_bf[:].rearrange("p (c i j) -> p c j i", i=4, j=4),
@@ -191,20 +154,67 @@ def tile_picked_unet_none_p_kernel(tc, x_words, x_scales, w1, w2, skip, offs, ce
         w2_scales = tile("w2_scales", [P, N], U8)
         nc.vector.quantize_mx(w2_codes[:].bitcast(FP8X4), w2_scales[:], w2_bf[:])
 
+        acc = bank("h2_first", "B3")
+        h_product(acc[:, :first], 2, 0, first)
+        h_scatter(2, 0, first, acc[:, :first])
+        acc = bank("h2_rest", "B0")
+        h_product(acc[:, :first], 2, first, half)
+        h_product(acc[:, first : first + half], 2, half, S)
+        h_scatter(2, first, S, acc[:, : S - first])
+        acc = bank("h1", "B1")
+        h_product(acc[:], 1, 0, S)
+        h_scatter(1, 0, S, acc[:], stage=tile("h_sb1", [P, S], F32, "raw_w2")[:, :])
+        acc3 = bank("h3", "B2")
+        h_product(acc3[:], 3, 0, S)
+        stage3 = tile("h_sb3", [P, S], F32)
+        nc.scalar.copy(stage3[:], acc3[:])
+
+        halves = [words[:, q, 1, :].bitcast(BF16).rearrange("p (v e) -> p v e", e=2) for q in range(4)]
+        for q in range(4):
+            cols = slice(q * QUARTER, (q + 1) * QUARTER)
+            nc.gpsimd.tensor_tensor(halves[q][:, :, 0], win[2][:, cols], words[:, q, 1, :], ADD)
+
+        zt = [tile(f"zt{q}", [P, 2, 2 * P], BF16) for q in range(4)]
+
+        def sum_transposed(w, blocks, tag):
+            total = bank(f"z{w}_{blocks[0]}", tag)
+            for source, opening in ((skip_sb[w], True), (win[w], False)):
+                for n, c in enumerate(blocks):
+                    nc.tensor.matmul(total[:, n * P : (n + 1) * P], lhsT=source[:, c * P : (c + 1) * P],
+                                     rhs=ident[:], is_transpose=True,
+                                     start=(opening and n == 0), stop=(not opening and n == len(blocks) - 1))
+            return total
+
+        for hf in range(2):
+            total = sum_transposed(0, list(range(4 * hf, 4 * hf + 4)), f"A{hf}")
+            for n in range(2):
+                nc.scalar.copy(zt[2 * hf + n][:, :, :P],
+                               total[:, n * QUARTER : (n + 1) * QUARTER].rearrange("p (c x) -> p c x", c=2))
+        for q, tag in enumerate(("C0", "C1", "B3", "B0")):
+            total = sum_transposed(1, [2 * q, 2 * q + 1], tag)
+            nc.scalar.copy(zt[q][:, :, P:], total[:, :QUARTER].rearrange("p (c x) -> p c x", c=2))
+        for q, tag in enumerate(("A0", "A1", "B1", "B2")):
+            back = bank(f"back{q}", tag)
+            for c in range(2):
+                nc.tensor.transpose(back[:, c * P : (c + 1) * P], zt[q][:, c, :].bitcast(F32), ident[:])
+            nc.scalar.copy(words[:, q, 0, :], back[:, :QUARTER])
+        nc.vector.tensor_copy(win[3][:].indirect(cell_t[:]), stage3[:])
+
         zq = [tile(f"zq{q}", [P, QUARTER * 4], BF16) for q in range(4)]
         for q in range(4):
             cols = slice(q * QUARTER, (q + 1) * QUARTER)
-            nc.vector.tensor_tensor(pairs[q][:, 1, :, 1], win[3][:, cols], skip23[:, 1, cols], ADD)
-        for q in range(4):
-            words = pairs[q][:].rearrange("p u v e -> p (u v e)").bitcast(F32)
-            nc.scalar.copy(zq[q][:].bitcast(F32).rearrange("p (v u) -> p v u", u=2), words.rearrange("p (u v) -> p v u", u=2))
+            nc.vector.tensor_tensor(halves[q][:, :, 1], win[3][:, cols], skip_sb[3][:, cols], ADD)
         pieces_out = [(0, 256), (256, 512), (512, 768), (768, 896), (896, 1024)]
+        for a, b in pieces_out:
+            q, at, width = a // QUARTER, a % QUARTER, b - a
+            nc.scalar.copy(zq[q][:].bitcast(F32).rearrange("p (v u) -> p v u", u=2)[:, at : at + width],
+                           words[:, q].rearrange("p u v -> p v u")[:, at : at + width])
         for n, (a, b) in enumerate(pieces_out):
             q, at, width = a // QUARTER, a % QUARTER, b - a
             z_codes = tile(f"z_codes{n}", [P, width], U32)
             z_scales = tile(f"z_scales{n}", [P, width], U8)
             nc.vector.quantize_mx(z_codes[:].bitcast(FP8X4), z_scales[:], zq[q][:, 4 * at : 4 * (at + width)])
-            res = bank(f"res{n}", ("B0", "B1", "B2", "B3", "C0")[n])
+            res = bank(f"res{n}", ("C0", "C1", "B3", "B0", "A0")[n])
             nc.tensor.matmul_mx(res[:, :width], lhsT=w2_codes[:].bitcast(FP8X4), lhsT_scale=w2_scales[:],
                                 rhs=z_codes[:].bitcast(FP8X4), rhs_scale=z_scales[:], start=True, stop=True)
             res_sb = tile(f"res_sb{n}", [P, width], F32)

@@ -35,50 +35,54 @@ def tile_picked_unet_none_p_kernel(tc, x_words, x_scales, w1, w2, skip, offs, ce
             return ps.tile([P, BANK], F32, name=name, tag=tag)
 
         offs_t = sb.tile([P, S // 16], U16, name="offs_t")
-        nc.sync.dma_start(offs_t[:], offs)
 
-        xw = [tile(f"xw{g}", [P, T], U32) for g in range(PASSES)]
+        cell_t = sb.tile([P, S // 16], U16, name="cell_t")
         w1_rows = w1.rearrange("(g p j) c -> g p j c", g=PASSES, j=4)
-        raw_lo = [tile(f"raw_lo{g}", [P, 4, 2 * P], F32) for g in range(PASSES)]
-        raw_hi = [tile(f"raw_hi{g}", [P, 4, 2 * P], F32) for g in range(PASSES)]
         xs = tile("xs", [P, T], U8)
-        nc.vector.memset(xs[:].bitcast(I32), 0)
-        xs_dram = x_scales.bitcast(I32)
+        xw = [tile("xw0", [P, T], U32), tile("xw1", [P, T], U32, "xs")]
+        raw_lo = [tile(f"raw_lo{g}", [P, 4, 2 * P], F32) for g in range(PASSES)]
+        gs = tile("gs", [P, S], U8)
+        nc.vector.memset(xs[32:64, :].bitcast(I32), 0)
+        nc.vector.memset(xs[64:, :].bitcast(I32), 0)
+        nc.vector.memset(gs[:].bitcast(I32), 0)
 
         def load_words(g):
             nc.sync.dma_start(xw[g][:].bitcast(I32), x_words[g].rearrange("p n t -> p (n t)").bitcast(I32))
 
+        nc.sync.dma_start(offs_t[:], offs)
+        nc.sync.dma_start(xs[:32, :].bitcast(I32), x_scales.rearrange("g r c -> (g r) c").bitcast(I32))
         load_words(0)
         nc.sync.dma_start(raw_lo[0][:], w1_rows[0, :, :, : 2 * P])
-        for q in range(4):
-            nc.sync.dma_start(xs[32 * q : 32 * q + 8, :].bitcast(I32), xs_dram[:, 4 * q : 4 * q + 4, :])
-        load_words(1)
-        nc.sync.dma_start(raw_lo[1][:], w1_rows[1, :, :, : 2 * P])
-        cell_t = sb.tile([P, S // 16], U16, name="cell_t")
         nc.sync.dma_start(cell_t[:], cell)
+        nc.sync.dma_start(raw_lo[1][:], w1_rows[1, :, :, : 2 * P])
+
+        picked_rows = tile("picked_rows", [P, S], U8)
+        nc.vector.tensor_copy(picked_rows[:], xs[:].indirect(offs_t[:]))
+
+        def place_scales(rows):
+            for g, q in rows:
+                src, dst = 16 * g + 4 * q, 32 * q + 4 * g
+                nc.sync.dma_start(gs[dst : dst + 4, :].bitcast(I32), picked_rows[src : src + 4, :].bitcast(I32))
+
+        scale_rows = [(g, q) for g in range(PASSES) for q in range(4)]
+        place_scales(scale_rows[:3])
+        load_words(1)
+        place_scales(scale_rows[3:])
+
+        raw_hi = [tile(f"raw_hi{g}", [P, 4, 2 * P], F32, ("xw0", "raw_lo0")[g]) for g in range(PASSES)]
         for g in range(PASSES):
             nc.sync.dma_start(raw_hi[g][:], w1_rows[g, :, :, 2 * P :])
-        raw_w2 = tile("raw_w2", [P, 4, N], F32)
-        nc.sync.dma_start(raw_w2[:], w2.rearrange("(p j) n -> p j n", j=4))
-        skip_rows = skip.rearrange("(p t) v -> p t v", t=4)
-        skip_sb = {w: tile(f"skip{w}", [P, U], F32) for w in (0, 1, 3)}
-        words = tile("words", [P, 4, 2, QUARTER], F32)
-        nc.sync.dma_start(skip_sb[0][:], skip_rows[:64, 0:2, :])
-        nc.sync.dma_start(skip_sb[1][:], skip_rows[64:, 0:2, :])
-        nc.sync.dma_start(words[:, :, 1, :], skip_rows[:, 2, :].rearrange("p (q v) -> p q v", q=4))
-        nc.sync.dma_start(skip_sb[3][:], skip_rows[:, 3, :])
-
         ident = tile("ident", [P, P], F32)
         make_identity(nc, ident[:])
         win = [tile(f"win{w}", [P, U], F32) for w in range(4)]
-        for w in range(4):
-            (nc.vector if w < 2 else nc.gpsimd).memset(win[w][:], 0.0)
+        nc.vector.memset(win[0][:], 0.0)
+        for w in (2, 1, 3):
+            nc.scalar.copy(win[w][:], win[0][:])
 
-        gs = tile("gs", [P, S], U8)
-        nc.vector.tensor_copy(gs[:], xs[:].indirect(offs_t[:]))
         gw = [tile(f"gw{g}", [P, S], U32) for g in range(PASSES)]
-        for g in range(PASSES):
-            nc.vector.tensor_copy(gw[g][:], xw[g][:].indirect(offs_t[:]))
+        nc.vector.tensor_copy(gw[0][:], xw[0][:].indirect(offs_t[:]))
+        for a in (0, S // 2):
+            nc.vector.tensor_copy(gw[1][:, a : a + S // 2], xw[1][:].indirect(offs_t[:, a // 16 : (a + S // 2) // 16]))
 
         bf23 = tile("w1_bf23", [P, 2, PASSES, P * 4], BF16)
         bf = [tile(f"w1_bf{w}", [P, PASSES, P * 4], BF16)[:, :, :] for w in range(2)] + [bf23[:, u] for u in range(2)]
@@ -88,8 +92,8 @@ def tile_picked_unet_none_p_kernel(tc, x_words, x_scales, w1, w2, skip, offs, ce
         def raw_part(g, part):
             return (raw_lo, raw_hi)[part][g][:].rearrange("p j (m t) -> p m j t", t=4)
 
-        def round_pairs(w, g, copy=nc.scalar.copy, a=0, b=64):
-            copy(bf[w][:, g].rearrange("p (m e j) -> p m j e", e=2, j=4)[:, a:b], raw_part(g, w)[:, a:b, :, 0:2])
+        def round_pairs(w, g):
+            nc.scalar.copy(bf[w][:, g].rearrange("p (m e j) -> p m j e", e=2, j=4), raw_part(g, w)[:, :, :, 0:2])
 
         def round_singles(g, part):
             nc.scalar.copy(bf23[:, :, g].rearrange("p u (m j) -> p m j u", j=4)[:, 64 * part : 64 * (part + 1)],
@@ -124,12 +128,18 @@ def tile_picked_unet_none_p_kernel(tc, x_words, x_scales, w1, w2, skip, offs, ce
 
         half = S // 2
         first = 128
-        round_pairs(0, 0)
-        quantize_w1(0, 0, 0, P)
-        round_singles(0, 0)
-        round_pairs(0, 1, nc.vector.tensor_copy, 0, 40)
-        round_pairs(0, 1, nc.scalar.copy, 40, 64)
-        quantize_w1(0, 1, 0, P)
+        for g in range(PASSES):
+            round_pairs(0, g)
+        quantize_window(0)
+        for g in range(PASSES):
+            round_singles(g, 0)
+        skip_rows = skip.rearrange("(p t) v -> p t v", t=4)
+        skip_sb = {0: tile("skip0", [P, U], F32, "raw_lo1")}
+        nc.sync.dma_start(skip_sb[0][:], skip_rows[:64, 0:2, :])
+        raw_w2 = tile("raw_w2", [P, 4, N], F32, "picked_rows")
+        nc.sync.dma_start(raw_w2[:], w2.rearrange("(p j) n -> p j n", j=4))
+        words = tile("words", [P, 4, 2, QUARTER], F32, "xs")
+        nc.sync.dma_start(words[:, :, 1, :], skip_rows[:, 2, :].rearrange("p (q v) -> p q v", q=4))
         cuts = (0, first, S - first, S)
         accs = []
         for n in range(3):
@@ -138,13 +148,16 @@ def tile_picked_unet_none_p_kernel(tc, x_words, x_scales, w1, w2, skip, offs, ce
             accs.append(acc)
         h_scatter(0, cuts[0], cuts[1], accs[0], copy=nc.vector.tensor_copy)
         h_scatter(0, cuts[1], cuts[2], accs[1])
-        round_singles(1, 0)
         round_singles(0, 1)
         round_pairs(1, 0)
+        skip_sb[1] = tile("skip1", [P, U], F32, "xw0")
+        nc.sync.dma_start(skip_sb[1][:], skip_rows[64:, 0:2, :])
         round_singles(1, 1)
         round_pairs(1, 1)
         quantize_window(1)
-        h_scatter(0, cuts[2], cuts[3], accs[2], stage=tile("h_sb0_last", [P, first], F32, "raw_hi1")[:, :])
+        h_scatter(0, cuts[2], cuts[3], accs[2], stage=tile("h_sb0_last", [P, first], F32, "raw_lo0")[:, :])
+        skip_sb[3] = tile("skip3", [P, U], F32, "raw_lo0")
+        nc.sync.dma_start(skip_sb[3][:], skip_rows[:, 3, :])
         w2_bf = tile("w2_bf", [P, N * 4], BF16)
         nc.scalar.copy(
             w2_bf[:].rearrange("p (c i j) -> p c j i", i=4, j=4),
@@ -163,10 +176,10 @@ def tile_picked_unet_none_p_kernel(tc, x_words, x_scales, w1, w2, skip, offs, ce
         h_scatter(2, first, S, acc[:, : S - first])
         acc = bank("h1", "B1")
         h_product(acc[:], 1, 0, S)
-        h_scatter(1, 0, S, acc[:], stage=tile("h_sb1", [P, S], F32, "raw_w2")[:, :])
-        acc3 = bank("h3", "B2")
+        h_scatter(1, 0, S, acc[:])
+        acc3 = bank("h3", "B1")
         h_product(acc3[:], 3, 0, S)
-        stage3 = tile("h_sb3", [P, S], F32)
+        stage3 = tile("h_sb3", [P, S], F32, "picked_rows")
         nc.scalar.copy(stage3[:], acc3[:])
 
         halves = [words[:, q, 1, :].bitcast(BF16).rearrange("p (v e) -> p v e", e=2) for q in range(4)]

@@ -158,7 +158,14 @@ def tile_picked_unet_none_p_kernel(tc, x_words, x_scales, w1, w2, skip, offs, ce
         h_scatter(0, cuts[2], cuts[3], accs[2], stage=tile("h_sb0_last", [P, first], F32, "raw_lo0")[:, :])
         skip_sb[3] = tile("skip3", [P, U], F32, "raw_lo0")
         nc.sync.dma_start(skip_sb[3][:], skip_rows[:, 3, :])
-        w2_bf = tile("w2_bf", [P, N * 4], BF16)
+        acc = bank("h2_first", "B3")
+        h_product(acc[:, :first], 2, 0, first)
+        h_scatter(2, 0, first, acc[:, :first])
+        acc = bank("h2_rest", "B4")
+        h_product(acc[:, :first], 2, first, half)
+        h_product(acc[:, first : first + half], 2, half, S)
+        h_scatter(2, first, S, acc[:, : S - first])
+        w2_bf = tile("w2_bf", [P, N * 4], BF16, "h_sb2_0")
         nc.scalar.copy(
             w2_bf[:].rearrange("p (c i j) -> p c j i", i=4, j=4),
             raw_w2[:].rearrange("p j (c i) -> p c j i", i=4),
@@ -166,18 +173,10 @@ def tile_picked_unet_none_p_kernel(tc, x_words, x_scales, w1, w2, skip, offs, ce
         w2_codes = tile("w2_codes", [P, N], U32)
         w2_scales = tile("w2_scales", [P, N], U8)
         nc.vector.quantize_mx(w2_codes[:].bitcast(FP8X4), w2_scales[:], w2_bf[:])
-
-        acc = bank("h2_first", "B3")
-        h_product(acc[:, :first], 2, 0, first)
-        h_scatter(2, 0, first, acc[:, :first])
-        acc = bank("h2_rest", "B0")
-        h_product(acc[:, :first], 2, first, half)
-        h_product(acc[:, first : first + half], 2, half, S)
-        h_scatter(2, first, S, acc[:, : S - first])
-        acc = bank("h1", "B1")
+        acc = bank("h1", "B5")
         h_product(acc[:], 1, 0, S)
         h_scatter(1, 0, S, acc[:])
-        acc3 = bank("h3", "B1")
+        acc3 = bank("h3", "B5")
         h_product(acc3[:], 3, 0, S)
         stage3 = tile("h_sb3", [P, S], F32, "picked_rows")
         nc.scalar.copy(stage3[:], acc3[:])
@@ -199,14 +198,14 @@ def tile_picked_unet_none_p_kernel(tc, x_words, x_scales, w1, w2, skip, offs, ce
             return total
 
         for hf in range(2):
-            total = sum_transposed(0, list(range(4 * hf, 4 * hf + 4)), f"A{hf}")
+            total = sum_transposed(0, list(range(4 * hf, 4 * hf + 4)), f"B{3 + hf}")
             for n in range(2):
                 nc.scalar.copy(zt[2 * hf + n][:, :, :P],
                                total[:, n * QUARTER : (n + 1) * QUARTER].rearrange("p (c x) -> p c x", c=2))
-        for q, tag in enumerate(("C0", "C1", "B3", "B0")):
+        for q, tag in enumerate(("B5", "B6", "B0", "B1")):
             total = sum_transposed(1, [2 * q, 2 * q + 1], tag)
             nc.scalar.copy(zt[q][:, :, P:], total[:, :QUARTER].rearrange("p (c x) -> p c x", c=2))
-        for q, tag in enumerate(("A0", "A1", "B1", "B2")):
+        for q, tag in enumerate(("B3", "B4", "B2", "B7")):
             back = bank(f"back{q}", tag)
             for c in range(2):
                 nc.tensor.transpose(back[:, c * P : (c + 1) * P], zt[q][:, c, :].bitcast(F32), ident[:])
@@ -227,7 +226,7 @@ def tile_picked_unet_none_p_kernel(tc, x_words, x_scales, w1, w2, skip, offs, ce
             z_codes = tile(f"z_codes{n}", [P, width], U32)
             z_scales = tile(f"z_scales{n}", [P, width], U8)
             nc.vector.quantize_mx(z_codes[:].bitcast(FP8X4), z_scales[:], zq[q][:, 4 * at : 4 * (at + width)])
-            res = bank(f"res{n}", ("C0", "C1", "B3", "B0", "A0")[n])
+            res = bank(f"res{n}", ("B5", "B6", "B0", "B1", "B3")[n])
             nc.tensor.matmul_mx(res[:, :width], lhsT=w2_codes[:].bitcast(FP8X4), lhsT_scale=w2_scales[:],
                                 rhs=z_codes[:].bitcast(FP8X4), rhs_scale=z_scales[:], start=True, stop=True)
             res_sb = tile(f"res_sb{n}", [P, width], F32)

@@ -16,10 +16,15 @@ FP8X4 = mybir.dt.float8_e4m3fn_x4
 ADD = mybir.AluOpType.add
 
 P = 128
-PASSES = 2
+PASSES = K // 512
 BANK = 512
-QUARTER = 256
 ALIGN = 64
+STRIPE = 16
+HALF = S // 2
+SHORT = 128
+QUARTER = U // 4
+ROWS_HALF = P // 2
+MOVES_AHEAD = 3
 
 
 def tile_picked_unet_none_p_kernel(tc, x_words, x_scales, w1, w2, skip, offs, cell, out):
@@ -31,12 +36,14 @@ def tile_picked_unet_none_p_kernel(tc, x_words, x_scales, w1, w2, skip, offs, ce
         def tile(name, shape, dtype, tag=None):
             return sb.tile(shape, dtype, name=name, tag=tag or name, align_bytes=ALIGN)
 
-        def bank(name, tag):
-            return ps.tile([P, BANK], F32, name=name, tag=tag)
+        def bank(name, number):
+            return ps.tile([P, BANK], F32, name=name, tag=f"B{number}")
 
-        offs_t = sb.tile([P, S // 16], U16, name="offs_t")
+        def entries(list_tile, a, b):
+            return list_tile[:, a // STRIPE : b // STRIPE]
 
-        cell_t = sb.tile([P, S // 16], U16, name="cell_t")
+        offs_t = sb.tile([P, S // STRIPE], U16, name="offs_t")
+        cell_t = sb.tile([P, S // STRIPE], U16, name="cell_t")
         w1_rows = w1.rearrange("(g p j) c -> g p j c", g=PASSES, j=4)
         xs = tile("xs", [P, T], U8)
         xw = [tile("xw0", [P, T], U32), tile("xw1", [P, T], U32, "xs")]
@@ -50,24 +57,24 @@ def tile_picked_unet_none_p_kernel(tc, x_words, x_scales, w1, w2, skip, offs, ce
             nc.sync.dma_start(xw[g][:].bitcast(I32), x_words[g].rearrange("p n t -> p (n t)").bitcast(I32))
 
         nc.sync.dma_start(offs_t[:], offs)
-        nc.sync.dma_start(xs[:32, :].bitcast(I32), x_scales.rearrange("g r c -> (g r) c").bitcast(I32))
+        nc.scalar.dma_start(xs[:32, :].bitcast(I32), x_scales.rearrange("g r c -> (g r) c").bitcast(I32))
         load_words(0)
-        nc.sync.dma_start(raw_lo[0][:], w1_rows[0, :, :, : 2 * P])
+        nc.scalar.dma_start(raw_lo[0][:], w1_rows[0, :, :, : 2 * P])
         nc.sync.dma_start(cell_t[:], cell)
-        nc.sync.dma_start(raw_lo[1][:], w1_rows[1, :, :, : 2 * P])
+        nc.scalar.dma_start(raw_lo[1][:], w1_rows[1, :, :, : 2 * P])
 
         picked_rows = tile("picked_rows", [P, S], U8)
         nc.vector.tensor_copy(picked_rows[:], xs[:].indirect(offs_t[:]))
 
-        def place_scales(rows):
-            for g, q in rows:
+        def place_scales(moves):
+            for g, q in moves:
                 src, dst = 16 * g + 4 * q, 32 * q + 4 * g
                 nc.sync.dma_start(gs[dst : dst + 4, :].bitcast(I32), picked_rows[src : src + 4, :].bitcast(I32))
 
-        scale_rows = [(g, q) for g in range(PASSES) for q in range(4)]
-        place_scales(scale_rows[:3])
+        all_moves = [(g, q) for g in range(PASSES) for q in range(4)]
+        place_scales(all_moves[:MOVES_AHEAD])
         load_words(1)
-        place_scales(scale_rows[3:])
+        place_scales(all_moves[MOVES_AHEAD:])
 
         raw_hi = [tile(f"raw_hi{g}", [P, 4, 2 * P], F32, ("xw0", "raw_lo0")[g]) for g in range(PASSES)]
         for g in range(PASSES):
@@ -81,8 +88,8 @@ def tile_picked_unet_none_p_kernel(tc, x_words, x_scales, w1, w2, skip, offs, ce
 
         gw = [tile(f"gw{g}", [P, S], U32) for g in range(PASSES)]
         nc.vector.tensor_copy(gw[0][:], xw[0][:].indirect(offs_t[:]))
-        for a in (0, S // 2):
-            nc.vector.tensor_copy(gw[1][:, a : a + S // 2], xw[1][:].indirect(offs_t[:, a // 16 : (a + S // 2) // 16]))
+        for a in (0, HALF):
+            nc.vector.tensor_copy(gw[1][:, a : a + HALF], xw[1][:].indirect(entries(offs_t, a, a + HALF)))
 
         bf23 = tile("w1_bf23", [P, 2, PASSES, P * 4], BF16)
         bf = [tile(f"w1_bf{w}", [P, PASSES, P * 4], BF16)[:, :, :] for w in range(2)] + [bf23[:, u] for u in range(2)]
@@ -92,21 +99,18 @@ def tile_picked_unet_none_p_kernel(tc, x_words, x_scales, w1, w2, skip, offs, ce
         def raw_part(g, part):
             return (raw_lo, raw_hi)[part][g][:].rearrange("p j (m t) -> p m j t", t=4)
 
-        def round_pairs(w, g):
+        def round_window01(w, g):
             nc.scalar.copy(bf[w][:, g].rearrange("p (m e j) -> p m j e", e=2, j=4), raw_part(g, w)[:, :, :, 0:2])
 
-        def round_singles(g, part):
-            nc.scalar.copy(bf23[:, :, g].rearrange("p u (m j) -> p m j u", j=4)[:, 64 * part : 64 * (part + 1)],
-                           raw_part(g, part)[:, :, :, 2:4])
-            for w in (2, 3):
-                quantize_w1(w, g, 64 * part, 64 * (part + 1))
-
-        def quantize_w1(w, g, a, b):
-            nc.vector.quantize_mx(codes[w][:, g, a:b].bitcast(FP8X4), scales[w][:, g, a:b], bf[w][:, g, 4 * a : 4 * b])
-
-        def quantize_window(w):
+        def quantize_window01(w):
             nc.vector.quantize_mx(codes[w][:].rearrange("p g m -> p (g m)").bitcast(FP8X4),
                                   scales[w][:].rearrange("p g m -> p (g m)"), bf[w].rearrange("p g x -> p (g x)"))
+
+        def round_and_quantize23(g, part):
+            a, b = ROWS_HALF * part, ROWS_HALF * (part + 1)
+            nc.scalar.copy(bf23[:, :, g].rearrange("p u (m j) -> p m j u", j=4)[:, a:b], raw_part(g, part)[:, :, :, 2:4])
+            for w in (2, 3):
+                nc.vector.quantize_mx(codes[w][:, g, a:b].bitcast(FP8X4), scales[w][:, g, a:b], bf[w][:, g, 4 * a : 4 * b])
 
         def h_product(acc, w, a, b):
             for g in range(PASSES):
@@ -120,76 +124,76 @@ def tile_picked_unet_none_p_kernel(tc, x_words, x_scales, w1, w2, skip, offs, ce
                     stop=(g == PASSES - 1),
                 )
 
-        def h_scatter(w, a, b, acc, copy=nc.scalar.copy, stage=None):
-            if stage is None:
-                stage = tile(f"h_sb{w}_{a}", [P, b - a], F32)[:, :]
-            copy(stage, acc)
-            nc.vector.tensor_copy(win[w][:].indirect(cell_t[:, a // 16 : b // 16]), stage)
+        def h_scatter(w, a, b, acc, copy=nc.scalar.copy, tag=None):
+            stage = tile(f"h_sb{w}_{a}", [P, b - a], F32, tag)
+            copy(stage[:], acc)
+            nc.vector.tensor_copy(win[w][:].indirect(entries(cell_t, a, b)), stage[:])
 
-        half = S // 2
-        first = 128
         for g in range(PASSES):
-            round_pairs(0, g)
-        quantize_window(0)
+            round_window01(0, g)
+        quantize_window01(0)
         for g in range(PASSES):
-            round_singles(g, 0)
+            round_and_quantize23(g, 0)
+
         skip_rows = skip.rearrange("(p t) v -> p t v", t=4)
         skip_sb = {0: tile("skip0", [P, U], F32, "raw_lo1")}
-        nc.sync.dma_start(skip_sb[0][:], skip_rows[:64, 0:2, :])
+        nc.sync.dma_start(skip_sb[0][:], skip_rows[:ROWS_HALF, 0:2, :])
         raw_w2 = tile("raw_w2", [P, 4, N], F32, "picked_rows")
         nc.sync.dma_start(raw_w2[:], w2.rearrange("(p j) n -> p j n", j=4))
-        words = tile("words", [P, 4, 2, QUARTER], F32, "xs")
-        nc.sync.dma_start(words[:, :, 1, :], skip_rows[:, 2, :].rearrange("p (q v) -> p q v", q=4))
-        cuts = (0, first, S - first, S)
+        pairs = tile("pairs", [P, 4, 2, QUARTER], F32, "xs")
+        nc.sync.dma_start(pairs[:, :, 1, :], skip_rows[:, 2, :].rearrange("p (q v) -> p q v", q=4))
+
+        cuts = (0, SHORT, S - SHORT, S)
         accs = []
         for n in range(3):
-            acc = bank(f"h0_{n}", f"B{n}")[:, : cuts[n + 1] - cuts[n]]
+            acc = bank(f"h0_{n}", n)[:, : cuts[n + 1] - cuts[n]]
             h_product(acc, 0, cuts[n], cuts[n + 1])
             accs.append(acc)
         h_scatter(0, cuts[0], cuts[1], accs[0], copy=nc.vector.tensor_copy)
         h_scatter(0, cuts[1], cuts[2], accs[1])
-        round_singles(0, 1)
-        round_pairs(1, 0)
+        round_and_quantize23(0, 1)
+        round_window01(1, 0)
         skip_sb[1] = tile("skip1", [P, U], F32, "xw0")
-        nc.sync.dma_start(skip_sb[1][:], skip_rows[64:, 0:2, :])
-        round_singles(1, 1)
-        round_pairs(1, 1)
-        quantize_window(1)
-        h_scatter(0, cuts[2], cuts[3], accs[2], stage=tile("h_sb0_last", [P, first], F32, "raw_lo0")[:, :])
+        nc.sync.dma_start(skip_sb[1][:], skip_rows[ROWS_HALF:, 0:2, :])
+        round_and_quantize23(1, 1)
+        round_window01(1, 1)
+        quantize_window01(1)
+        h_scatter(0, cuts[2], cuts[3], accs[2], tag="raw_lo0")
         skip_sb[3] = tile("skip3", [P, U], F32, "raw_lo0")
         nc.sync.dma_start(skip_sb[3][:], skip_rows[:, 3, :])
-        acc = bank("h2_first", "B3")
-        h_product(acc[:, :first], 2, 0, first)
-        h_scatter(2, 0, first, acc[:, :first])
-        acc = bank("h2_rest", "B4")
-        h_product(acc[:, :first], 2, first, half)
-        h_product(acc[:, first : first + half], 2, half, S)
-        h_scatter(2, first, S, acc[:, : S - first])
+
+        acc = bank("h2_first", 3)
+        h_product(acc[:, :SHORT], 2, 0, SHORT)
+        h_scatter(2, 0, SHORT, acc[:, :SHORT])
+        acc = bank("h2_rest", 4)
+        h_product(acc[:, :SHORT], 2, SHORT, HALF)
+        h_product(acc[:, SHORT : SHORT + HALF], 2, HALF, S)
+        h_scatter(2, SHORT, S, acc[:, : S - SHORT])
         w2_bf = tile("w2_bf", [P, N * 4], BF16, "h_sb2_0")
         nc.scalar.copy(
-            w2_bf[:].rearrange("p (c i j) -> p c j i", i=4, j=4),
-            raw_w2[:].rearrange("p j (c i) -> p c j i", i=4),
+            w2_bf[:].rearrange("p (c n j) -> p c j n", n=4, j=4),
+            raw_w2[:].rearrange("p j (c n) -> p c j n", n=4),
         )
         w2_codes = tile("w2_codes", [P, N], U32)
         w2_scales = tile("w2_scales", [P, N], U8)
         nc.vector.quantize_mx(w2_codes[:].bitcast(FP8X4), w2_scales[:], w2_bf[:])
-        acc = bank("h1", "B5")
+        acc = bank("h1", 5)
         h_product(acc[:], 1, 0, S)
         h_scatter(1, 0, S, acc[:])
-        acc3 = bank("h3", "B5")
-        h_product(acc3[:], 3, 0, S)
+        acc = bank("h3", 5)
+        h_product(acc[:], 3, 0, S)
         stage3 = tile("h_sb3", [P, S], F32, "picked_rows")
-        nc.scalar.copy(stage3[:], acc3[:])
+        nc.scalar.copy(stage3[:], acc[:])
 
-        halves = [words[:, q, 1, :].bitcast(BF16).rearrange("p (v e) -> p v e", e=2) for q in range(4)]
+        halves = [pairs[:, q, 1, :].bitcast(BF16).rearrange("p (v e) -> p v e", e=2) for q in range(4)]
         for q in range(4):
             cols = slice(q * QUARTER, (q + 1) * QUARTER)
-            nc.gpsimd.tensor_tensor(halves[q][:, :, 0], win[2][:, cols], words[:, q, 1, :], ADD)
+            nc.gpsimd.tensor_tensor(halves[q][:, :, 0], win[2][:, cols], pairs[:, q, 1, :], ADD)
 
         zt = [tile(f"zt{q}", [P, 2, 2 * P], BF16) for q in range(4)]
 
-        def sum_transposed(w, blocks, tag):
-            total = bank(f"z{w}_{blocks[0]}", tag)
+        def sum_transposed(w, blocks, number):
+            total = bank(f"z{w}_{blocks[0]}", number)
             for source, opening in ((skip_sb[w], True), (win[w], False)):
                 for n, c in enumerate(blocks):
                     nc.tensor.matmul(total[:, n * P : (n + 1) * P], lhsT=source[:, c * P : (c + 1) * P],
@@ -198,38 +202,41 @@ def tile_picked_unet_none_p_kernel(tc, x_words, x_scales, w1, w2, skip, offs, ce
             return total
 
         for hf in range(2):
-            total = sum_transposed(0, list(range(4 * hf, 4 * hf + 4)), f"B{3 + hf}")
+            total = sum_transposed(0, list(range(4 * hf, 4 * hf + 4)), 3 + hf)
             for n in range(2):
                 nc.scalar.copy(zt[2 * hf + n][:, :, :P],
                                total[:, n * QUARTER : (n + 1) * QUARTER].rearrange("p (c x) -> p c x", c=2))
-        for q, tag in enumerate(("B5", "B6", "B0", "B1")):
-            total = sum_transposed(1, [2 * q, 2 * q + 1], tag)
+        banks_there, banks_back = (5, 6, 0, 1), (3, 4, 2, 7)
+        for q in range(4):
+            total = sum_transposed(1, [2 * q, 2 * q + 1], banks_there[q])
             nc.scalar.copy(zt[q][:, :, P:], total[:, :QUARTER].rearrange("p (c x) -> p c x", c=2))
-        for q, tag in enumerate(("B3", "B4", "B2", "B7")):
-            back = bank(f"back{q}", tag)
+        for q in range(4):
+            back = bank(f"back{q}", banks_back[q])
             for c in range(2):
                 nc.tensor.transpose(back[:, c * P : (c + 1) * P], zt[q][:, c, :].bitcast(F32), ident[:])
-            nc.scalar.copy(words[:, q, 0, :], back[:, :QUARTER])
-        nc.vector.tensor_copy(win[3][:].indirect(cell_t[:]), stage3[:])
+            nc.scalar.copy(pairs[:, q, 0, :], back[:, :QUARTER])
 
+        nc.vector.tensor_copy(win[3][:].indirect(cell_t[:]), stage3[:])
         zq = [tile(f"zq{q}", [P, QUARTER * 4], BF16) for q in range(4)]
         for q in range(4):
             cols = slice(q * QUARTER, (q + 1) * QUARTER)
             nc.vector.tensor_tensor(halves[q][:, :, 1], win[3][:, cols], skip_sb[3][:, cols], ADD)
-        pieces_out = [(0, 256), (256, 512), (512, 768), (768, 896), (896, 1024)]
-        for a, b in pieces_out:
+        edges = (0, QUARTER, 2 * QUARTER, 3 * QUARTER, U - QUARTER // 2, U)
+        pieces = list(zip(edges[:-1], edges[1:]))
+        for a, b in pieces:
             q, at, width = a // QUARTER, a % QUARTER, b - a
             nc.scalar.copy(zq[q][:].bitcast(F32).rearrange("p (v u) -> p v u", u=2)[:, at : at + width],
-                           words[:, q].rearrange("p u v -> p v u")[:, at : at + width])
-        for n, (a, b) in enumerate(pieces_out):
+                           pairs[:, q].rearrange("p u v -> p v u")[:, at : at + width])
+        banks_out = banks_there + banks_back[:1]
+        for n, (a, b) in enumerate(pieces):
             q, at, width = a // QUARTER, a % QUARTER, b - a
             z_codes = tile(f"z_codes{n}", [P, width], U32)
             z_scales = tile(f"z_scales{n}", [P, width], U8)
             nc.vector.quantize_mx(z_codes[:].bitcast(FP8X4), z_scales[:], zq[q][:, 4 * at : 4 * (at + width)])
-            res = bank(f"res{n}", ("B5", "B6", "B0", "B1", "B3")[n])
+            res = bank(f"res{n}", banks_out[n])
             nc.tensor.matmul_mx(res[:, :width], lhsT=w2_codes[:].bitcast(FP8X4), lhsT_scale=w2_scales[:],
                                 rhs=z_codes[:].bitcast(FP8X4), rhs_scale=z_scales[:], start=True, stop=True)
             res_sb = tile(f"res_sb{n}", [P, width], F32)
-            copy = nc.vector.tensor_copy if n == len(pieces_out) - 1 else nc.scalar.copy
+            copy = nc.vector.tensor_copy if n == len(pieces) - 1 else nc.scalar.copy
             copy(res_sb[:], res[:, :width])
             nc.sync.dma_start(out[:, a:b], res_sb[:])

@@ -143,47 +143,40 @@ def tile_picked_unet_none_p_kernel(tc, x_words, x_scales, w1, w2, skip, offs, ce
         pairs = tile("pairs", [P, 4, 2, QUARTER], F32, "xs")
         nc.sync.dma_start(pairs[:, :, 1, :], skip_rows[:, 2, :].rearrange("p (q v) -> p q v", q=4))
 
-        cuts = (0, SHORT, S - SHORT, S)
         accs = []
-        for n in range(3):
-            acc = bank(f"h0_{n}", n)[:, : cuts[n + 1] - cuts[n]]
-            h_product(acc, 0, cuts[n], cuts[n + 1])
+        for n in range(2):
+            acc = bank(f"h0_{n}", n)[:, :HALF]
+            h_product(acc, 0, n * HALF, (n + 1) * HALF)
             accs.append(acc)
-        h_scatter(0, cuts[0], cuts[1], accs[0], copy=nc.vector.tensor_copy)
-        h_scatter(0, cuts[1], cuts[2], accs[1])
+        h_scatter(0, 0, HALF, accs[0], copy=nc.vector.tensor_copy)
         round_and_quantize23(0, 1)
         round_window01(1, 0)
+        round_and_quantize23(1, 1)
+        h_scatter(0, HALF, S, accs[1], tag="xw0")
         skip_sb[1] = tile("skip1", [P, U], F32, "xw0")
         nc.sync.dma_start(skip_sb[1][:], skip_rows[ROWS_HALF:, 0:2, :])
-        round_and_quantize23(1, 1)
         round_window01(1, 1)
         quantize_window01(1)
-        h_scatter(0, cuts[2], cuts[3], accs[2], tag="raw_lo0")
         skip_sb[3] = tile("skip3", [P, U], F32, "raw_lo0")
         nc.sync.dma_start(skip_sb[3][:], skip_rows[:, 3, :])
 
-        acc = bank("h2_first", 3)
-        h_product(acc[:, :SHORT], 2, 0, SHORT)
-        h_scatter(2, 0, SHORT, acc[:, :SHORT])
-        acc = bank("h2_rest", 4)
-        h_product(acc[:, :SHORT], 2, SHORT, HALF)
-        h_product(acc[:, SHORT : SHORT + HALF], 2, HALF, S)
-        h_scatter(2, SHORT, S, acc[:, : S - SHORT])
-        w2_bf = tile("w2_bf", [P, N * 4], BF16, "h_sb2_0")
+        acc = bank("h2", 3)
+        h_product(acc[:], 2, 0, S)
+        h_scatter(2, 0, S, acc[:])
+        acc = bank("h1", 5)
+        h_product(acc[:], 1, 0, S)
+        h_scatter(1, 0, S, acc[:])
+        acc = bank("h3", 4)
+        h_product(acc[:], 3, 0, S)
+        stage3 = tile("h_sb3", [P, S], F32, "w1_codes1")
+        nc.scalar.copy(stage3[:], acc[:])
+        w2_bf = tile("w2_bf", [P, N * 4], BF16, "h_sb1_0")
         nc.scalar.copy(
             w2_bf[:].rearrange("p (c n j) -> p c j n", n=4, j=4),
             raw_w2[:].rearrange("p j (c n) -> p c j n", n=4),
         )
         w2_codes = tile("w2_codes", [P, N], U32)
         w2_scales = tile("w2_scales", [P, N], U8)
-        nc.vector.quantize_mx(w2_codes[:].bitcast(FP8X4), w2_scales[:], w2_bf[:])
-        acc = bank("h1", 5)
-        h_product(acc[:], 1, 0, S)
-        h_scatter(1, 0, S, acc[:])
-        acc = bank("h3", 5)
-        h_product(acc[:], 3, 0, S)
-        stage3 = tile("h_sb3", [P, S], F32, "picked_rows")
-        nc.scalar.copy(stage3[:], acc[:])
 
         halves = [pairs[:, q, 1, :].bitcast(BF16).rearrange("p (v e) -> p v e", e=2) for q in range(4)]
         for q in range(4):
@@ -217,6 +210,7 @@ def tile_picked_unet_none_p_kernel(tc, x_words, x_scales, w1, w2, skip, offs, ce
             nc.scalar.copy(pairs[:, q, 0, :], back[:, :QUARTER])
 
         nc.vector.tensor_copy(win[3][:].indirect(cell_t[:]), stage3[:])
+        nc.vector.quantize_mx(w2_codes[:].bitcast(FP8X4), w2_scales[:], w2_bf[:])
         zq = [tile(f"zq{q}", [P, QUARTER * 4], BF16) for q in range(4)]
         for q in range(4):
             cols = slice(q * QUARTER, (q + 1) * QUARTER)
@@ -228,6 +222,7 @@ def tile_picked_unet_none_p_kernel(tc, x_words, x_scales, w1, w2, skip, offs, ce
             nc.scalar.copy(zq[q][:].bitcast(F32).rearrange("p (v u) -> p v u", u=2)[:, at : at + width],
                            pairs[:, q].rearrange("p u v -> p v u")[:, at : at + width])
         banks_out = banks_there + banks_back[:1]
+        res_early = tile("res_early", [P, 3 * QUARTER], F32, "xs")
         for n, (a, b) in enumerate(pieces):
             q, at, width = a // QUARTER, a % QUARTER, b - a
             z_codes = tile(f"z_codes{n}", [P, width], U32)
@@ -236,7 +231,10 @@ def tile_picked_unet_none_p_kernel(tc, x_words, x_scales, w1, w2, skip, offs, ce
             res = bank(f"res{n}", banks_out[n])
             nc.tensor.matmul_mx(res[:, :width], lhsT=w2_codes[:].bitcast(FP8X4), lhsT_scale=w2_scales[:],
                                 rhs=z_codes[:].bitcast(FP8X4), rhs_scale=z_scales[:], start=True, stop=True)
-            res_sb = tile(f"res_sb{n}", [P, width], F32)
-            copy = nc.vector.tensor_copy if n == len(pieces) - 1 else nc.scalar.copy
-            copy(res_sb[:], res[:, :width])
-            nc.sync.dma_start(out[:, a:b], res_sb[:])
+            if n < 3:
+                res_sb = res_early[:, a:b]
+                nc.scalar.copy(res_sb, res[:, :width])
+            else:
+                res_sb = tile(f"res_sb{n}", [P, width], F32)[:, :]
+                nc.vector.tensor_copy(res_sb, res[:, :width])
+            nc.sync.dma_start(out[:, a:b], res_sb)

@@ -211,7 +211,8 @@ def tile_picked_unet_none_p_kernel(tc, x_words, x_scales, w1, w2, skip, offs, ce
 
         nc.vector.tensor_copy(win[3][:].indirect(cell_t[:]), stage3[:])
         nc.vector.quantize_mx(w2_codes[:].bitcast(FP8X4), w2_scales[:], w2_bf[:])
-        zq = [tile(f"zq{q}", [P, QUARTER * 4], BF16) for q in range(4)]
+        zq_all = tile("zq", [P, U * 4], BF16, "zt3")
+        zq = [zq_all[:, 4 * QUARTER * q : 4 * QUARTER * (q + 1)] for q in range(4)]
         for q in range(4):
             cols = slice(q * QUARTER, (q + 1) * QUARTER)
             nc.vector.tensor_tensor(halves[q][:, :, 1], win[3][:, cols], skip_sb[3][:, cols], ADD)
@@ -219,10 +220,10 @@ def tile_picked_unet_none_p_kernel(tc, x_words, x_scales, w1, w2, skip, offs, ce
         pieces = list(zip(edges[:-1], edges[1:]))
         for a, b in pieces:
             q, at, width = a // QUARTER, a % QUARTER, b - a
-            nc.scalar.copy(zq[q][:].bitcast(F32).rearrange("p (v u) -> p v u", u=2)[:, at : at + width],
+            nc.scalar.copy(zq[q].bitcast(F32).rearrange("p (v u) -> p v u", u=2)[:, at : at + width],
                            pairs[:, q].rearrange("p u v -> p v u")[:, at : at + width])
         banks_out = banks_there + banks_back[:1]
-        res_early = tile("res_early", [P, 3 * QUARTER], F32, "xs")
+        res_early = tile("res_early", [P, 2 * QUARTER], F32, "xs")
         for n, (a, b) in enumerate(pieces):
             q, at, width = a // QUARTER, a % QUARTER, b - a
             z_codes = tile(f"z_codes{n}", [P, width], U32)
@@ -231,7 +232,7 @@ def tile_picked_unet_none_p_kernel(tc, x_words, x_scales, w1, w2, skip, offs, ce
             res = bank(f"res{n}", banks_out[n])
             nc.tensor.matmul_mx(res[:, :width], lhsT=w2_codes[:].bitcast(FP8X4), lhsT_scale=w2_scales[:],
                                 rhs=z_codes[:].bitcast(FP8X4), rhs_scale=z_scales[:], start=True, stop=True)
-            if n < 3:
+            if n < 2:
                 res_sb = res_early[:, a:b]
                 nc.scalar.copy(res_sb, res[:, :width])
             else:

@@ -23,6 +23,7 @@ STRIPE = 16
 HALF = S // 2
 SHORT = 128
 QUARTER = U // 4
+RAW = 4 * 2 * P
 ROWS_HALF = P // 2
 MOVES_AHEAD = 3
 
@@ -76,9 +77,10 @@ def tile_picked_unet_none_p_kernel(tc, x_words, x_scales, w1, w2, skip, offs, ce
         load_words(1)
         place_scales(all_moves[MOVES_AHEAD:])
 
-        raw_hi = [tile(f"raw_hi{g}", [P, 4, 2 * P], F32, ("xw0", "raw_lo0")[g]) for g in range(PASSES)]
+        hi_row = tile("hi_row", [P, PASSES * RAW + HALF], F32, "xw0")
+        raw_hi = [hi_row[:, g * RAW : (g + 1) * RAW].rearrange("p (j c) -> p j c", j=4) for g in range(PASSES)]
         for g in range(PASSES):
-            nc.sync.dma_start(raw_hi[g][:], w1_rows[g, :, :, 2 * P :])
+            nc.sync.dma_start(raw_hi[g], w1_rows[g, :, :, 2 * P :])
         ident = tile("ident", [P, P], F32)
         make_identity(nc, ident[:])
         win = [tile(f"win{w}", [P, U], F32) for w in range(4)]
@@ -97,7 +99,7 @@ def tile_picked_unet_none_p_kernel(tc, x_words, x_scales, w1, w2, skip, offs, ce
         scales = [tile(f"w1_scales{w}", [P, PASSES, P], U8) for w in range(4)]
 
         def raw_part(g, part):
-            return (raw_lo, raw_hi)[part][g][:].rearrange("p j (m t) -> p m j t", t=4)
+            return (raw_lo[g][:], raw_hi[g])[part].rearrange("p j (m t) -> p m j t", t=4)
 
         def round_window01(w, g):
             nc.scalar.copy(bf[w][:, g].rearrange("p (m e j) -> p m j e", e=2, j=4), raw_part(g, w)[:, :, :, 0:2])
@@ -106,11 +108,18 @@ def tile_picked_unet_none_p_kernel(tc, x_words, x_scales, w1, w2, skip, offs, ce
             nc.vector.quantize_mx(codes[w][:].rearrange("p g m -> p (g m)").bitcast(FP8X4),
                                   scales[w][:].rearrange("p g m -> p (g m)"), bf[w].rearrange("p g x -> p (g x)"))
 
-        def round_and_quantize23(g, part):
+        def round23(g, part):
             a, b = ROWS_HALF * part, ROWS_HALF * (part + 1)
             nc.scalar.copy(bf23[:, :, g].rearrange("p u (m j) -> p m j u", j=4)[:, a:b], raw_part(g, part)[:, :, :, 2:4])
+
+        def quantize23(g, part):
+            a, b = ROWS_HALF * part, ROWS_HALF * (part + 1)
             for w in (2, 3):
                 nc.vector.quantize_mx(codes[w][:, g, a:b].bitcast(FP8X4), scales[w][:, g, a:b], bf[w][:, g, 4 * a : 4 * b])
+
+        def round_and_quantize23(g, part):
+            round23(g, part)
+            quantize23(g, part)
 
         def h_product(acc, w, a, b):
             for g in range(PASSES):
@@ -140,29 +149,40 @@ def tile_picked_unet_none_p_kernel(tc, x_words, x_scales, w1, w2, skip, offs, ce
         nc.sync.dma_start(skip_sb[0][:], skip_rows[:ROWS_HALF, 0:2, :])
         raw_w2 = tile("raw_w2", [P, 4, N], F32, "picked_rows")
         nc.sync.dma_start(raw_w2[:], w2.rearrange("(p j) n -> p j n", j=4))
-        pairs = tile("pairs", [P, 4, 2, QUARTER], F32, "xs")
-        nc.sync.dma_start(pairs[:, :, 1, :], skip_rows[:, 2, :].rearrange("p (q v) -> p q v", q=4))
+        pairs = tile("pairs", [P, 2 * U], F32, "xs")
+        nc.sync.dma_start(pairs[:, U:], skip_rows[:, 2, :])
 
+        cuts = (0, SHORT, HALF, S)
         accs = []
-        for n in range(2):
-            acc = bank(f"h0_{n}", n)[:, :HALF]
-            h_product(acc, 0, n * HALF, (n + 1) * HALF)
+        for n in range(3):
+            acc = bank(f"h0_{n}", n)[:, : cuts[n + 1] - cuts[n]]
+            h_product(acc, 0, cuts[n], cuts[n + 1])
             accs.append(acc)
-        h_scatter(0, 0, HALF, accs[0], copy=nc.vector.tensor_copy)
+        stage = tile("h_sb0_0", [P, HALF], F32)
+        nc.scalar.copy(stage[:, :SHORT], accs[0])
+        nc.vector.tensor_copy(stage[:, SHORT:], accs[1])
+        nc.vector.tensor_copy(win[0][:].indirect(entries(cell_t, 0, HALF)), stage[:])
         round_and_quantize23(0, 1)
-        round_window01(1, 0)
-        round_and_quantize23(1, 1)
-        h_scatter(0, HALF, S, accs[1], tag="xw0")
+        stage = hi_row[:, PASSES * RAW - 2 : PASSES * RAW - 2 + HALF]
+        nc.scalar.copy(stage[:, 2:], accs[2][:, 2:])
+        round23(1, 1)
+        nc.vector.tensor_copy(stage[:, :2], accs[2][:, :2])
+        quantize23(1, 1)
+        nc.vector.tensor_copy(win[0][:].indirect(entries(cell_t, HALF, S)), stage)
+        nc.scalar.copy(bf[1].rearrange("p g (m e j) -> p g m j e", e=2, j=4),
+                       hi_row[:, : PASSES * RAW].rearrange("p (g j m t) -> p g m j t", g=PASSES, j=4, t=4)[:, :, :, :, 0:2])
+        quantize_window01(1)
         skip_sb[1] = tile("skip1", [P, U], F32, "xw0")
         nc.sync.dma_start(skip_sb[1][:], skip_rows[ROWS_HALF:, 0:2, :])
-        round_window01(1, 1)
-        quantize_window01(1)
-        skip_sb[3] = tile("skip3", [P, U], F32, "raw_lo0")
-        nc.sync.dma_start(skip_sb[3][:], skip_rows[:, 3, :])
 
-        acc = bank("h2", 3)
-        h_product(acc[:], 2, 0, S)
-        h_scatter(2, 0, S, acc[:])
+        stage = tile("h_sb2", [P, S], F32)
+        for n in range(2):
+            acc = bank(f"h2_{n}", (3, 7)[n])[:, :HALF]
+            h_product(acc, 2, n * HALF, (n + 1) * HALF)
+            nc.scalar.copy(stage[:, n * HALF : (n + 1) * HALF], acc)
+        nc.vector.tensor_copy(win[2][:].indirect(cell_t[:]), stage[:])
+        skip_sb[3] = tile("skip3", [P, U], F32, "h_sb2")
+        nc.sync.dma_start(skip_sb[3][:], skip_rows[:, 3, :])
         acc = bank("h1", 5)
         h_product(acc[:], 1, 0, S)
         h_scatter(1, 0, S, acc[:])
@@ -178,10 +198,10 @@ def tile_picked_unet_none_p_kernel(tc, x_words, x_scales, w1, w2, skip, offs, ce
         w2_codes = tile("w2_codes", [P, N], U32)
         w2_scales = tile("w2_scales", [P, N], U8)
 
-        halves = [pairs[:, q, 1, :].bitcast(BF16).rearrange("p (v e) -> p v e", e=2) for q in range(4)]
-        for q in range(4):
-            cols = slice(q * QUARTER, (q + 1) * QUARTER)
-            nc.gpsimd.tensor_tensor(halves[q][:, :, 0], win[2][:, cols], pairs[:, q, 1, :], ADD)
+        halves = pairs[:, U:].bitcast(BF16).rearrange("p (v e) -> p v e", e=2)
+        for a in range(0, U, QUARTER):
+            b = a + QUARTER
+            nc.gpsimd.tensor_tensor(halves[:, a:b, 0], win[2][:, a:b], pairs[:, U + a : U + b], ADD)
 
         zt = [tile(f"zt{q}", [P, 2, 2 * P], BF16) for q in range(4)]
 
@@ -207,32 +227,29 @@ def tile_picked_unet_none_p_kernel(tc, x_words, x_scales, w1, w2, skip, offs, ce
             back = bank(f"back{q}", banks_back[q])
             for c in range(2):
                 nc.tensor.transpose(back[:, c * P : (c + 1) * P], zt[q][:, c, :].bitcast(F32), ident[:])
-            nc.scalar.copy(pairs[:, q, 0, :], back[:, :QUARTER])
+            nc.scalar.copy(pairs[:, q * QUARTER : (q + 1) * QUARTER], back[:, :QUARTER])
 
         nc.vector.tensor_copy(win[3][:].indirect(cell_t[:]), stage3[:])
         nc.vector.quantize_mx(w2_codes[:].bitcast(FP8X4), w2_scales[:], w2_bf[:])
-        zq_all = tile("zq", [P, U * 4], BF16, "zt3")
-        zq = [zq_all[:, 4 * QUARTER * q : 4 * QUARTER * (q + 1)] for q in range(4)]
-        for q in range(4):
-            cols = slice(q * QUARTER, (q + 1) * QUARTER)
-            nc.vector.tensor_tensor(halves[q][:, :, 1], win[3][:, cols], skip_sb[3][:, cols], ADD)
-        edges = (0, QUARTER, 2 * QUARTER, 3 * QUARTER, U - QUARTER // 2, U)
+        zq = tile("zq", [P, U * 4], BF16, "zt3")
+        edges = (0, SHORT, SHORT + QUARTER, SHORT + 2 * QUARTER, U - SHORT, U)
         pieces = list(zip(edges[:-1], edges[1:]))
         for a, b in pieces:
-            q, at, width = a // QUARTER, a % QUARTER, b - a
-            nc.scalar.copy(zq[q].bitcast(F32).rearrange("p (v u) -> p v u", u=2)[:, at : at + width],
-                           pairs[:, q].rearrange("p u v -> p v u")[:, at : at + width])
+            nc.vector.tensor_tensor(halves[:, a:b, 1], win[3][:, a:b], skip_sb[3][:, a:b], ADD)
+        for a, b in pieces:
+            nc.scalar.copy(zq[:].bitcast(F32).rearrange("p (v u) -> p v u", u=2)[:, a:b],
+                           pairs[:].rearrange("p (u v) -> p v u", u=2)[:, a:b])
         banks_out = banks_there + banks_back[:1]
-        res_early = tile("res_early", [P, 2 * QUARTER], F32, "xs")
+        res_early = tile("res_early", [P, edges[3]], F32, "xs")
         for n, (a, b) in enumerate(pieces):
-            q, at, width = a // QUARTER, a % QUARTER, b - a
+            width = b - a
             z_codes = tile(f"z_codes{n}", [P, width], U32)
             z_scales = tile(f"z_scales{n}", [P, width], U8)
-            nc.vector.quantize_mx(z_codes[:].bitcast(FP8X4), z_scales[:], zq[q][:, 4 * at : 4 * (at + width)])
+            nc.vector.quantize_mx(z_codes[:].bitcast(FP8X4), z_scales[:], zq[:, 4 * a : 4 * b])
             res = bank(f"res{n}", banks_out[n])
             nc.tensor.matmul_mx(res[:, :width], lhsT=w2_codes[:].bitcast(FP8X4), lhsT_scale=w2_scales[:],
                                 rhs=z_codes[:].bitcast(FP8X4), rhs_scale=z_scales[:], start=True, stop=True)
-            if n < 2:
+            if n < 3:
                 res_sb = res_early[:, a:b]
                 nc.scalar.copy(res_sb, res[:, :width])
             else:

@@ -199,9 +199,7 @@ def tile_picked_unet_none_p_kernel(tc, x_words, x_scales, w1, w2, skip, offs, ce
         w2_scales = tile("w2_scales", [P, N], U8)
 
         halves = pairs[:, U:].bitcast(BF16).rearrange("p (v e) -> p v e", e=2)
-        for a in range(0, U, QUARTER):
-            b = a + QUARTER
-            nc.gpsimd.tensor_tensor(halves[:, a:b, 0], win[2][:, a:b], pairs[:, U + a : U + b], ADD)
+        nc.gpsimd.tensor_tensor(halves[:, :, 0], win[2][:], pairs[:, U:], ADD)
 
         zt = [tile(f"zt{q}", [P, 2, 2 * P], BF16) for q in range(4)]
 
@@ -232,15 +230,16 @@ def tile_picked_unet_none_p_kernel(tc, x_words, x_scales, w1, w2, skip, offs, ce
         nc.vector.tensor_copy(win[3][:].indirect(cell_t[:]), stage3[:])
         nc.vector.quantize_mx(w2_codes[:].bitcast(FP8X4), w2_scales[:], w2_bf[:])
         zq = tile("zq", [P, U * 4], BF16, "zt3")
-        edges = (0, SHORT, SHORT + QUARTER, SHORT + 2 * QUARTER, U - SHORT, U)
+        edges = (0, SHORT, SHORT + QUARTER, SHORT + 2 * QUARTER, U - 2 * SHORT, U - SHORT, U)
         pieces = list(zip(edges[:-1], edges[1:]))
         for a, b in pieces:
             nc.vector.tensor_tensor(halves[:, a:b, 1], win[3][:, a:b], skip_sb[3][:, a:b], ADD)
         for a, b in pieces:
             nc.scalar.copy(zq[:].bitcast(F32).rearrange("p (v u) -> p v u", u=2)[:, a:b],
                            pairs[:].rearrange("p (u v) -> p v u", u=2)[:, a:b])
-        banks_out = banks_there + banks_back[:1]
+        banks_out = banks_there + banks_back[:2]
         res_early = tile("res_early", [P, edges[3]], F32, "xs")
+        res_late = tile("res_late", [P, U - edges[3]], F32)
         for n, (a, b) in enumerate(pieces):
             width = b - a
             z_codes = tile(f"z_codes{n}", [P, width], U32)
@@ -250,9 +249,10 @@ def tile_picked_unet_none_p_kernel(tc, x_words, x_scales, w1, w2, skip, offs, ce
             nc.tensor.matmul_mx(res[:, :width], lhsT=w2_codes[:].bitcast(FP8X4), lhsT_scale=w2_scales[:],
                                 rhs=z_codes[:].bitcast(FP8X4), rhs_scale=z_scales[:], start=True, stop=True)
             if n < 3:
-                res_sb = res_early[:, a:b]
-                nc.scalar.copy(res_sb, res[:, :width])
+                nc.scalar.copy(res_early[:, a:b], res[:, :width])
             else:
-                res_sb = tile(f"res_sb{n}", [P, width], F32)[:, :]
-                nc.vector.tensor_copy(res_sb, res[:, :width])
-            nc.sync.dma_start(out[:, a:b], res_sb)
+                nc.vector.tensor_copy(res_late[:, a - edges[3] : b - edges[3]], res[:, :width])
+            if n < 3:
+                (nc.scalar if n == 2 else nc.sync).dma_start(out[:, a:b], res_early[:, a:b])
+            else:
+                nc.sync.dma_start(out[:, a:b], res_late[:, a - edges[3] : b - edges[3]])

@@ -24,8 +24,10 @@ HALF = S // 2
 SHORT = 128
 QUARTER = U // 4
 RAW = 4 * 2 * P
+HELD = 2
 ROWS_HALF = P // 2
 MOVES_AHEAD = 3
+ON_SCALAR = 4
 
 
 def tile_picked_unet_none_p_kernel(tc, x_words, x_scales, w1, w2, skip, offs, cell, out):
@@ -101,9 +103,6 @@ def tile_picked_unet_none_p_kernel(tc, x_words, x_scales, w1, w2, skip, offs, ce
         def raw_part(g, part):
             return (raw_lo[g][:], raw_hi[g])[part].rearrange("p j (m t) -> p m j t", t=4)
 
-        def round_window01(w, g):
-            nc.scalar.copy(bf[w][:, g].rearrange("p (m e j) -> p m j e", e=2, j=4), raw_part(g, w)[:, :, :, 0:2])
-
         def quantize_window01(w):
             nc.vector.quantize_mx(codes[w][:].rearrange("p g m -> p (g m)").bitcast(FP8X4),
                                   scales[w][:].rearrange("p g m -> p (g m)"), bf[w].rearrange("p g x -> p (g x)"))
@@ -133,13 +132,8 @@ def tile_picked_unet_none_p_kernel(tc, x_words, x_scales, w1, w2, skip, offs, ce
                     stop=(g == PASSES - 1),
                 )
 
-        def h_scatter(w, a, b, acc, copy=nc.scalar.copy, tag=None):
-            stage = tile(f"h_sb{w}_{a}", [P, b - a], F32, tag)
-            copy(stage[:], acc)
-            nc.vector.tensor_copy(win[w][:].indirect(entries(cell_t, a, b)), stage[:])
-
         for g in range(PASSES):
-            round_window01(0, g)
+            nc.scalar.copy(bf[0][:, g].rearrange("p (m e j) -> p m j e", e=2, j=4), raw_part(g, 0)[:, :, :, 0:2])
         quantize_window01(0)
         for g in range(PASSES):
             round_and_quantize23(g, 0)
@@ -154,38 +148,40 @@ def tile_picked_unet_none_p_kernel(tc, x_words, x_scales, w1, w2, skip, offs, ce
 
         cuts = (0, SHORT, HALF, S)
         accs = []
-        for n in range(3):
+        for n in range(len(cuts) - 1):
             acc = bank(f"h0_{n}", n)[:, : cuts[n + 1] - cuts[n]]
             h_product(acc, 0, cuts[n], cuts[n + 1])
             accs.append(acc)
-        stage = tile("h_sb0_0", [P, HALF], F32)
-        nc.scalar.copy(stage[:, :SHORT], accs[0])
-        nc.vector.tensor_copy(stage[:, SHORT:], accs[1])
-        nc.vector.tensor_copy(win[0][:].indirect(entries(cell_t, 0, HALF)), stage[:])
+        stage0_first = tile("h_sb0_0", [P, HALF], F32)
+        nc.scalar.copy(stage0_first[:, :SHORT], accs[0])
+        nc.vector.tensor_copy(stage0_first[:, SHORT:], accs[1])
+        nc.vector.tensor_copy(win[0][:].indirect(entries(cell_t, 0, HALF)), stage0_first[:])
         round_and_quantize23(0, 1)
-        stage = hi_row[:, PASSES * RAW - 2 : PASSES * RAW - 2 + HALF]
-        nc.scalar.copy(stage[:, 2:], accs[2][:, 2:])
+        stage0_second = hi_row[:, PASSES * RAW - HELD : PASSES * RAW - HELD + HALF]
+        nc.scalar.copy(stage0_second[:, HELD:], accs[2][:, HELD:])
         round23(1, 1)
-        nc.vector.tensor_copy(stage[:, :2], accs[2][:, :2])
+        nc.vector.tensor_copy(stage0_second[:, :HELD], accs[2][:, :HELD])
         quantize23(1, 1)
-        nc.vector.tensor_copy(win[0][:].indirect(entries(cell_t, HALF, S)), stage)
+        nc.vector.tensor_copy(win[0][:].indirect(entries(cell_t, HALF, S)), stage0_second)
         nc.scalar.copy(bf[1].rearrange("p g (m e j) -> p g m j e", e=2, j=4),
                        hi_row[:, : PASSES * RAW].rearrange("p (g j m t) -> p g m j t", g=PASSES, j=4, t=4)[:, :, :, :, 0:2])
         quantize_window01(1)
         skip_sb[1] = tile("skip1", [P, U], F32, "xw0")
         nc.sync.dma_start(skip_sb[1][:], skip_rows[ROWS_HALF:, 0:2, :])
 
-        stage = tile("h_sb2", [P, S], F32)
+        stage2 = tile("h_sb2", [P, S], F32)
         for n in range(2):
             acc = bank(f"h2_{n}", (3, 7)[n])[:, :HALF]
             h_product(acc, 2, n * HALF, (n + 1) * HALF)
-            nc.scalar.copy(stage[:, n * HALF : (n + 1) * HALF], acc)
-        nc.vector.tensor_copy(win[2][:].indirect(cell_t[:]), stage[:])
+            nc.scalar.copy(stage2[:, n * HALF : (n + 1) * HALF], acc)
+        nc.vector.tensor_copy(win[2][:].indirect(cell_t[:]), stage2[:])
         skip_sb[3] = tile("skip3", [P, U], F32, "h_sb2")
         nc.sync.dma_start(skip_sb[3][:], skip_rows[:, 3, :])
         acc = bank("h1", 5)
         h_product(acc[:], 1, 0, S)
-        h_scatter(1, 0, S, acc[:])
+        stage1 = tile("h_sb1_0", [P, S], F32)
+        nc.scalar.copy(stage1[:], acc[:])
+        nc.vector.tensor_copy(win[1][:].indirect(cell_t[:]), stage1[:])
         acc = bank("h3", 4)
         h_product(acc[:], 3, 0, S)
         stage3 = tile("h_sb3", [P, S], F32, "w1_codes1")
@@ -203,24 +199,26 @@ def tile_picked_unet_none_p_kernel(tc, x_words, x_scales, w1, w2, skip, offs, ce
 
         zt = [tile(f"zt{q}", [P, 2, 2 * P], BF16) for q in range(4)]
 
-        def sum_transposed(w, blocks, number):
-            total = bank(f"z{w}_{blocks[0]}", number)
-            for source, opening in ((skip_sb[w], True), (win[w], False)):
-                for n, c in enumerate(blocks):
-                    nc.tensor.matmul(total[:, n * P : (n + 1) * P], lhsT=source[:, c * P : (c + 1) * P],
-                                     rhs=ident[:], is_transpose=True,
-                                     start=(opening and n == 0), stop=(not opening and n == len(blocks) - 1))
-            return total
+        def add_transposed(total, source, blocks, opening):
+            for n, c in enumerate(blocks):
+                nc.tensor.matmul(total[:, n * P : (n + 1) * P], lhsT=source[:, c * P : (c + 1) * P],
+                                 rhs=ident[:], is_transpose=True,
+                                 start=(opening and n == 0), stop=(not opening and n == len(blocks) - 1))
 
         for hf in range(2):
-            total = sum_transposed(0, list(range(4 * hf, 4 * hf + 4)), 3 + hf)
+            total = bank(f"z0_{hf}", 3 + hf)
+            add_transposed(total, skip_sb[0], range(4 * hf, 4 * hf + 4), True)
+            add_transposed(total, win[0], range(4 * hf, 4 * hf + 4), False)
             for n in range(2):
                 nc.scalar.copy(zt[2 * hf + n][:, :, :P],
                                total[:, n * QUARTER : (n + 1) * QUARTER].rearrange("p (c x) -> p c x", c=2))
         banks_there, banks_back = (5, 6, 0, 1), (3, 4, 2, 7)
+        totals = [bank(f"z1_{q}", banks_there[q]) for q in range(4)]
         for q in range(4):
-            total = sum_transposed(1, [2 * q, 2 * q + 1], banks_there[q])
-            nc.scalar.copy(zt[q][:, :, P:], total[:, :QUARTER].rearrange("p (c x) -> p c x", c=2))
+            add_transposed(totals[q], skip_sb[1], (2 * q, 2 * q + 1), True)
+        for q in range(4):
+            add_transposed(totals[q], win[1], (2 * q, 2 * q + 1), False)
+            nc.scalar.copy(zt[q][:, :, P:], totals[q][:, :QUARTER].rearrange("p (c x) -> p c x", c=2))
         for q in range(4):
             back = bank(f"back{q}", banks_back[q])
             for c in range(2):
@@ -238,8 +236,8 @@ def tile_picked_unet_none_p_kernel(tc, x_words, x_scales, w1, w2, skip, offs, ce
             nc.scalar.copy(zq[:].bitcast(F32).rearrange("p (v u) -> p v u", u=2)[:, a:b],
                            pairs[:].rearrange("p (u v) -> p v u", u=2)[:, a:b])
         banks_out = banks_there + banks_back[:2]
-        res_early = tile("res_early", [P, edges[3]], F32, "xs")
-        res_late = tile("res_late", [P, U - edges[3]], F32)
+        res_early = tile("res_early", [P, edges[ON_SCALAR]], F32, "xs")
+        res_late = tile("res_late", [P, U - edges[ON_SCALAR]], F32)
         for n, (a, b) in enumerate(pieces):
             width = b - a
             z_codes = tile(f"z_codes{n}", [P, width], U32)
@@ -248,11 +246,9 @@ def tile_picked_unet_none_p_kernel(tc, x_words, x_scales, w1, w2, skip, offs, ce
             res = bank(f"res{n}", banks_out[n])
             nc.tensor.matmul_mx(res[:, :width], lhsT=w2_codes[:].bitcast(FP8X4), lhsT_scale=w2_scales[:],
                                 rhs=z_codes[:].bitcast(FP8X4), rhs_scale=z_scales[:], start=True, stop=True)
-            if n < 3:
+            if n < ON_SCALAR:
                 nc.scalar.copy(res_early[:, a:b], res[:, :width])
+                (nc.scalar if n == ON_SCALAR - 1 else nc.sync).dma_start(out[:, a:b], res_early[:, a:b])
             else:
-                nc.vector.tensor_copy(res_late[:, a - edges[3] : b - edges[3]], res[:, :width])
-            if n < 3:
-                (nc.scalar if n == 2 else nc.sync).dma_start(out[:, a:b], res_early[:, a:b])
-            else:
-                nc.sync.dma_start(out[:, a:b], res_late[:, a - edges[3] : b - edges[3]])
+                nc.vector.tensor_copy(res_late[:, a - edges[ON_SCALAR] : b - edges[ON_SCALAR]], res[:, :width])
+                nc.sync.dma_start(out[:, a:b], res_late[:, a - edges[ON_SCALAR] : b - edges[ON_SCALAR]])

@@ -14,6 +14,7 @@ U16 = mybir.dt.uint16
 U8 = mybir.dt.uint8
 FP8X4 = mybir.dt.float8_e4m3fn_x4
 ADD = mybir.AluOpType.add
+COPY = mybir.ActivationFunctionType.Copy
 
 P = 128
 PASSES = K // 512
@@ -24,7 +25,6 @@ HALF = S // 2
 SHORT = 128
 QUARTER = U // 4
 RAW = 4 * 2 * P
-HELD = 2
 ROWS_HALF = P // 2
 MOVES_AHEAD = 3
 ON_SCALAR = 4
@@ -79,7 +79,7 @@ def tile_picked_unet_none_p_kernel(tc, x_words, x_scales, w1, w2, skip, offs, ce
         load_words(1)
         place_scales(all_moves[MOVES_AHEAD:])
 
-        hi_row = tile("hi_row", [P, PASSES * RAW + HALF], F32, "xw0")
+        hi_row = tile("hi_row", [P, PASSES * RAW], F32, "xw0")
         raw_hi = [hi_row[:, g * RAW : (g + 1) * RAW].rearrange("p (j c) -> p j c", j=4) for g in range(PASSES)]
         for g in range(PASSES):
             nc.sync.dma_start(raw_hi[g], w1_rows[g, :, :, 2 * P :])
@@ -92,8 +92,8 @@ def tile_picked_unet_none_p_kernel(tc, x_words, x_scales, w1, w2, skip, offs, ce
 
         gw = [tile(f"gw{g}", [P, S], U32) for g in range(PASSES)]
         nc.vector.tensor_copy(gw[0][:], xw[0][:].indirect(offs_t[:]))
-        for a in (0, HALF):
-            nc.vector.tensor_copy(gw[1][:, a : a + HALF], xw[1][:].indirect(entries(offs_t, a, a + HALF)))
+        for a, b in ((0, SHORT), (SHORT, HALF), (HALF, S)):
+            nc.vector.tensor_copy(gw[1][:, a:b], xw[1][:].indirect(entries(offs_t, a, b)))
 
         bf23 = tile("w1_bf23", [P, 2, PASSES, P * 4], BF16)
         bf = [tile(f"w1_bf{w}", [P, PASSES, P * 4], BF16)[:, :, :] for w in range(2)] + [bf23[:, u] for u in range(2)]
@@ -107,18 +107,16 @@ def tile_picked_unet_none_p_kernel(tc, x_words, x_scales, w1, w2, skip, offs, ce
             nc.vector.quantize_mx(codes[w][:].rearrange("p g m -> p (g m)").bitcast(FP8X4),
                                   scales[w][:].rearrange("p g m -> p (g m)"), bf[w].rearrange("p g x -> p (g x)"))
 
-        def round23(g, part):
-            a, b = ROWS_HALF * part, ROWS_HALF * (part + 1)
-            nc.scalar.copy(bf23[:, :, g].rearrange("p u (m j) -> p m j u", j=4)[:, a:b], raw_part(g, part)[:, :, :, 2:4])
+        def round01(copy, g, part):
+            copy(bf[part][:, g].rearrange("p (m e j) -> p m j e", e=2, j=4), raw_part(g, part)[:, :, :, 0:2])
 
-        def quantize23(g, part):
+        def round23(copy, g, part):
             a, b = ROWS_HALF * part, ROWS_HALF * (part + 1)
-            for w in (2, 3):
-                nc.vector.quantize_mx(codes[w][:, g, a:b].bitcast(FP8X4), scales[w][:, g, a:b], bf[w][:, g, 4 * a : 4 * b])
+            copy(bf23[:, :, g].rearrange("p u (m j) -> p m j u", j=4)[:, a:b], raw_part(g, part)[:, :, :, 2:4])
 
-        def round_and_quantize23(g, part):
-            round23(g, part)
-            quantize23(g, part)
+        def quantize_half(w, g, part):
+            a, b = ROWS_HALF * part, ROWS_HALF * (part + 1)
+            nc.vector.quantize_mx(codes[w][:, g, a:b].bitcast(FP8X4), scales[w][:, g, a:b], bf[w][:, g, 4 * a : 4 * b])
 
         def h_product(acc, w, a, b):
             for g in range(PASSES):
@@ -133,10 +131,12 @@ def tile_picked_unet_none_p_kernel(tc, x_words, x_scales, w1, w2, skip, offs, ce
                 )
 
         for g in range(PASSES):
-            nc.scalar.copy(bf[0][:, g].rearrange("p (m e j) -> p m j e", e=2, j=4), raw_part(g, 0)[:, :, :, 0:2])
+            round01(nc.scalar.copy, g, 0)
         quantize_window01(0)
         for g in range(PASSES):
-            round_and_quantize23(g, 0)
+            round23(nc.scalar.copy, g, 0)
+            for w in (2, 3):
+                quantize_half(w, g, 0)
 
         skip_rows = skip.rearrange("(p t) v -> p t v", t=4)
         skip_sb = {0: tile("skip0", [P, U], F32, "raw_lo1")}
@@ -146,48 +146,50 @@ def tile_picked_unet_none_p_kernel(tc, x_words, x_scales, w1, w2, skip, offs, ce
         pairs = tile("pairs", [P, 2 * U], F32, "xs")
         nc.sync.dma_start(pairs[:, U:], skip_rows[:, 2, :])
 
-        cuts = (0, SHORT, HALF, S)
-        accs = []
-        for n in range(len(cuts) - 1):
-            acc = bank(f"h0_{n}", n)[:, : cuts[n + 1] - cuts[n]]
-            h_product(acc, 0, cuts[n], cuts[n + 1])
-            accs.append(acc)
-        stage0_first = tile("h_sb0_0", [P, HALF], F32)
-        nc.scalar.copy(stage0_first[:, :SHORT], accs[0])
-        nc.vector.tensor_copy(stage0_first[:, SHORT:], accs[1])
-        nc.vector.tensor_copy(win[0][:].indirect(entries(cell_t, 0, HALF)), stage0_first[:])
-        round_and_quantize23(0, 1)
-        stage0_second = hi_row[:, PASSES * RAW - HELD : PASSES * RAW - HELD + HALF]
-        nc.scalar.copy(stage0_second[:, HELD:], accs[2][:, HELD:])
-        round23(1, 1)
-        nc.vector.tensor_copy(stage0_second[:, :HELD], accs[2][:, :HELD])
-        quantize23(1, 1)
-        nc.vector.tensor_copy(win[0][:].indirect(entries(cell_t, HALF, S)), stage0_second)
-        nc.scalar.copy(bf[1].rearrange("p g (m e j) -> p g m j e", e=2, j=4),
-                       hi_row[:, : PASSES * RAW].rearrange("p (g j m t) -> p g m j t", g=PASSES, j=4, t=4)[:, :, :, :, 0:2])
+        def product(name, number, w, a, b):
+            acc = bank(name, number)[:, : b - a]
+            h_product(acc, w, a, b)
+            return acc
+
+        def on_scalar(w, stage, a, b):
+            nc.scalar.activation(win[w][:].indirect(entries(cell_t, a, b)), stage, COPY)
+
+        def on_vector(w, stage, a, b):
+            nc.vector.tensor_copy(win[w][:].indirect(entries(cell_t, a, b)), stage)
+
+        stage0 = tile("h_sb0", [P, S], F32)
+        nc.scalar.copy(stage0[:, :SHORT], product("h0_0", 0, 0, 0, SHORT))
+        on_scalar(0, stage0[:, :SHORT], 0, SHORT)
+        nc.scalar.copy(stage0[:, SHORT:HALF], product("h0_1", 1, 0, SHORT, HALF))
+        nc.scalar.copy(stage0[:, HALF:], product("h0_2", 2, 0, HALF, S))
+        on_scalar(0, stage0[:, SHORT:], SHORT, S)
+        round23(nc.vector.tensor_copy, 0, 1)
+        round01(nc.vector.tensor_copy, 0, 1)
+        quantize_half(2, 0, 1)
+        round23(nc.vector.tensor_copy, 1, 1)
+        quantize_half(3, 0, 1)
+        quantize_half(2, 1, 1)
+        round01(nc.vector.tensor_copy, 1, 1)
+        quantize_half(3, 1, 1)
         quantize_window01(1)
         skip_sb[1] = tile("skip1", [P, U], F32, "xw0")
         nc.sync.dma_start(skip_sb[1][:], skip_rows[ROWS_HALF:, 0:2, :])
 
-        stage2 = tile("h_sb2", [P, S], F32)
-        for n in range(2):
-            acc = bank(f"h2_{n}", (3, 7)[n])[:, :HALF]
-            h_product(acc, 2, n * HALF, (n + 1) * HALF)
-            nc.scalar.copy(stage2[:, n * HALF : (n + 1) * HALF], acc)
-        nc.vector.tensor_copy(win[2][:].indirect(cell_t[:]), stage2[:])
-        skip_sb[3] = tile("skip3", [P, U], F32, "h_sb2")
+        stage2 = [tile(f"h_sb2_{n}", [P, HALF], F32) for n in range(2)]
+        nc.vector.tensor_copy(stage2[0][:], product("h2_0", 3, 2, 0, HALF))
+        on_vector(2, stage2[0][:], 0, HALF)
+        stage1 = tile("h_sb1", [P, S], F32)
+        nc.scalar.copy(stage1[:], product("h1", 5, 1, 0, S))
+        nc.vector.tensor_copy(stage2[1][:], product("h2_1", 7, 2, HALF, S))
+        on_vector(2, stage2[1][:], HALF, S)
+        on_scalar(1, stage1[:, :HALF], 0, HALF)
+        on_scalar(1, stage1[:, HALF:], HALF, S)
+        skip_sb[3] = tile("skip3", [P, U], F32, "h_sb2_1")
         nc.sync.dma_start(skip_sb[3][:], skip_rows[:, 3, :])
-        acc = bank("h1", 5)
-        h_product(acc[:], 1, 0, S)
-        stage1 = tile("h_sb1_0", [P, S], F32)
-        nc.scalar.copy(stage1[:], acc[:])
-        nc.vector.tensor_copy(win[1][:].indirect(cell_t[:]), stage1[:])
-        acc = bank("h3", 4)
-        h_product(acc[:], 3, 0, S)
-        stage3 = tile("h_sb3", [P, S], F32, "w1_codes1")
-        nc.scalar.copy(stage3[:], acc[:])
-        w2_bf = tile("w2_bf", [P, N * 4], BF16, "h_sb1_0")
-        nc.scalar.copy(
+        stage3 = tile("h_sb3", [P, S], F32)
+        nc.vector.tensor_copy(stage3[:], product("h3", 4, 3, 0, S))
+        w2_bf = tile("w2_bf", [P, N * 4], BF16, "h_sb2_0")
+        nc.vector.tensor_copy(
             w2_bf[:].rearrange("p (c n j) -> p c j n", n=4, j=4),
             raw_w2[:].rearrange("p j (c n) -> p c j n", n=4),
         )
@@ -197,7 +199,8 @@ def tile_picked_unet_none_p_kernel(tc, x_words, x_scales, w1, w2, skip, offs, ce
         halves = pairs[:, U:].bitcast(BF16).rearrange("p (v e) -> p v e", e=2)
         nc.gpsimd.tensor_tensor(halves[:, :, 0], win[2][:], pairs[:, U:], ADD)
 
-        zt = [tile(f"zt{q}", [P, 2, 2 * P], BF16) for q in range(4)]
+        zt_half = [tile(f"zt{hf}", [P, 4, 2 * P], BF16) for hf in range(2)]
+        zt = [zt_half[q // 2][:, 2 * (q % 2) : 2 * (q % 2) + 2] for q in range(4)]
 
         def add_transposed(total, source, blocks, opening):
             for n, c in enumerate(blocks):
@@ -206,13 +209,11 @@ def tile_picked_unet_none_p_kernel(tc, x_words, x_scales, w1, w2, skip, offs, ce
                                  start=(opening and n == 0), stop=(not opening and n == len(blocks) - 1))
 
         for hf in range(2):
-            total = bank(f"z0_{hf}", 3 + hf)
+            total = bank(f"z0_{hf}", 5 + hf)
             add_transposed(total, skip_sb[0], range(4 * hf, 4 * hf + 4), True)
             add_transposed(total, win[0], range(4 * hf, 4 * hf + 4), False)
-            for n in range(2):
-                nc.scalar.copy(zt[2 * hf + n][:, :, :P],
-                               total[:, n * QUARTER : (n + 1) * QUARTER].rearrange("p (c x) -> p c x", c=2))
-        banks_there, banks_back = (5, 6, 0, 1), (3, 4, 2, 7)
+            nc.scalar.copy(zt_half[hf][:, :, :P], total[:].rearrange("p (c x) -> p c x", c=4))
+        banks_there, banks_back = (0, 1, 2, 3), (7, 4, 5, 6)
         totals = [bank(f"z1_{q}", banks_there[q]) for q in range(4)]
         for q in range(4):
             add_transposed(totals[q], skip_sb[1], (2 * q, 2 * q + 1), True)
@@ -227,7 +228,7 @@ def tile_picked_unet_none_p_kernel(tc, x_words, x_scales, w1, w2, skip, offs, ce
 
         nc.vector.tensor_copy(win[3][:].indirect(cell_t[:]), stage3[:])
         nc.vector.quantize_mx(w2_codes[:].bitcast(FP8X4), w2_scales[:], w2_bf[:])
-        zq = tile("zq", [P, U * 4], BF16, "zt3")
+        zq = tile("zq", [P, U * 4], BF16, "zt1")
         edges = (0, SHORT, SHORT + QUARTER, SHORT + 2 * QUARTER, U - 2 * SHORT, U - SHORT, U)
         pieces = list(zip(edges[:-1], edges[1:]))
         for a, b in pieces:

@@ -27,7 +27,7 @@ QUARTER = U // 4
 RAW = 4 * 2 * P
 ROWS_HALF = P // 2
 MOVES_AHEAD = 3
-ON_SCALAR = 4
+ON_SCALAR = 5
 
 
 def tile_picked_unet_none_p_kernel(tc, x_words, x_scales, w1, w2, skip, offs, cell, out):
@@ -143,8 +143,9 @@ def tile_picked_unet_none_p_kernel(tc, x_words, x_scales, w1, w2, skip, offs, ce
         nc.sync.dma_start(skip_sb[0][:], skip_rows[:ROWS_HALF, 0:2, :])
         raw_w2 = tile("raw_w2", [P, 4, N], F32, "picked_rows")
         nc.sync.dma_start(raw_w2[:], w2.rearrange("(p j) n -> p j n", j=4))
-        pairs = tile("pairs", [P, 2 * U], F32, "xs")
-        nc.sync.dma_start(pairs[:, U:], skip_rows[:, 2, :])
+        pairs = tile("pairs", [P, 2 * U], F32)
+        skip_sb[2] = tile("skip2", [P, U], F32, "xs")
+        nc.sync.dma_start(skip_sb[2][:], skip_rows[:, 2, :])
 
         def product(name, number, w, a, b):
             acc = bank(name, number)[:, : b - a]
@@ -182,12 +183,12 @@ def tile_picked_unet_none_p_kernel(tc, x_words, x_scales, w1, w2, skip, offs, ce
         nc.scalar.copy(stage1[:], product("h1", 5, 1, 0, S))
         nc.vector.tensor_copy(stage2[1][:], product("h2_1", 7, 2, HALF, S))
         on_vector(2, stage2[1][:], HALF, S)
+        stage3 = tile("h_sb3", [P, S], F32)
+        nc.scalar.copy(stage3[:], product("h3", 4, 3, 0, S))
         on_scalar(1, stage1[:, :HALF], 0, HALF)
         on_scalar(1, stage1[:, HALF:], HALF, S)
         skip_sb[3] = tile("skip3", [P, U], F32, "h_sb2_1")
         nc.sync.dma_start(skip_sb[3][:], skip_rows[:, 3, :])
-        stage3 = tile("h_sb3", [P, S], F32)
-        nc.vector.tensor_copy(stage3[:], product("h3", 4, 3, 0, S))
         w2_bf = tile("w2_bf", [P, N * 4], BF16, "h_sb2_0")
         nc.vector.tensor_copy(
             w2_bf[:].rearrange("p (c n j) -> p c j n", n=4, j=4),
@@ -197,7 +198,7 @@ def tile_picked_unet_none_p_kernel(tc, x_words, x_scales, w1, w2, skip, offs, ce
         w2_scales = tile("w2_scales", [P, N], U8)
 
         halves = pairs[:, U:].bitcast(BF16).rearrange("p (v e) -> p v e", e=2)
-        nc.gpsimd.tensor_tensor(halves[:, :, 0], win[2][:], pairs[:, U:], ADD)
+        nc.vector.tensor_tensor(halves[:, :, 0], win[2][:], skip_sb[2][:], ADD)
 
         zt_half = [tile(f"zt{hf}", [P, 4, 2 * P], BF16) for hf in range(2)]
         zt = [zt_half[q // 2][:, 2 * (q % 2) : 2 * (q % 2) + 2] for q in range(4)]
@@ -237,7 +238,7 @@ def tile_picked_unet_none_p_kernel(tc, x_words, x_scales, w1, w2, skip, offs, ce
             nc.scalar.copy(zq[:].bitcast(F32).rearrange("p (v u) -> p v u", u=2)[:, a:b],
                            pairs[:].rearrange("p (u v) -> p v u", u=2)[:, a:b])
         banks_out = banks_there + banks_back[:2]
-        res_early = tile("res_early", [P, edges[ON_SCALAR]], F32, "xs")
+        res_early = tile("res_early", [P, edges[ON_SCALAR]], F32, "pairs")
         res_late = tile("res_late", [P, U - edges[ON_SCALAR]], F32)
         for n, (a, b) in enumerate(pieces):
             width = b - a

@@ -27,7 +27,7 @@ QUARTER = U // 4
 RAW = 4 * 2 * P
 ROWS_HALF = P // 2
 MOVES_AHEAD = 3
-ON_SCALAR = 5
+ON_VECTOR = (2, 3)
 
 
 def tile_picked_unet_none_p_kernel(tc, x_words, x_scales, w1, w2, skip, offs, cell, out):
@@ -50,7 +50,9 @@ def tile_picked_unet_none_p_kernel(tc, x_words, x_scales, w1, w2, skip, offs, ce
         w1_rows = w1.rearrange("(g p j) c -> g p j c", g=PASSES, j=4)
         xs = tile("xs", [P, T], U8)
         xw = [tile("xw0", [P, T], U32), tile("xw1", [P, T], U32, "xs")]
-        raw_lo = [tile(f"raw_lo{g}", [P, 4, 2 * P], F32) for g in range(PASSES)]
+        win = [tile(f"win{w}", [P, U * (1 + w // 2)], F32) for w in range(4)]
+        raw_lo = [win[2][:, U:], tile("raw_lo1", [P, RAW], F32)[:, :]]
+        raw_lo = [r.rearrange("p (j c) -> p j c", j=4) for r in raw_lo]
         gs = tile("gs", [P, S], U8)
         nc.vector.memset(xs[32:64, :].bitcast(I32), 0)
         nc.vector.memset(xs[64:, :].bitcast(I32), 0)
@@ -62,9 +64,9 @@ def tile_picked_unet_none_p_kernel(tc, x_words, x_scales, w1, w2, skip, offs, ce
         nc.sync.dma_start(offs_t[:], offs)
         nc.scalar.dma_start(xs[:32, :].bitcast(I32), x_scales.rearrange("g r c -> (g r) c").bitcast(I32))
         load_words(0)
-        nc.scalar.dma_start(raw_lo[0][:], w1_rows[0, :, :, : 2 * P])
+        nc.scalar.dma_start(raw_lo[0], w1_rows[0, :, :, : 2 * P])
         nc.sync.dma_start(cell_t[:], cell)
-        nc.scalar.dma_start(raw_lo[1][:], w1_rows[1, :, :, : 2 * P])
+        nc.scalar.dma_start(raw_lo[1], w1_rows[1, :, :, : 2 * P])
 
         picked_rows = tile("picked_rows", [P, S], U8)
         nc.vector.tensor_copy(picked_rows[:], xs[:].indirect(offs_t[:]))
@@ -85,10 +87,9 @@ def tile_picked_unet_none_p_kernel(tc, x_words, x_scales, w1, w2, skip, offs, ce
             nc.sync.dma_start(raw_hi[g], w1_rows[g, :, :, 2 * P :])
         ident = tile("ident", [P, P], F32)
         make_identity(nc, ident[:])
-        win = [tile(f"win{w}", [P, U], F32) for w in range(4)]
         nc.vector.memset(win[0][:], 0.0)
         for w in (2, 1, 3):
-            nc.scalar.copy(win[w][:], win[0][:])
+            nc.scalar.copy(win[w][:, :U], win[0][:])
 
         gw = [tile(f"gw{g}", [P, S], U32) for g in range(PASSES)]
         nc.vector.tensor_copy(gw[0][:], xw[0][:].indirect(offs_t[:]))
@@ -101,7 +102,7 @@ def tile_picked_unet_none_p_kernel(tc, x_words, x_scales, w1, w2, skip, offs, ce
         scales = [tile(f"w1_scales{w}", [P, PASSES, P], U8) for w in range(4)]
 
         def raw_part(g, part):
-            return (raw_lo[g][:], raw_hi[g])[part].rearrange("p j (m t) -> p m j t", t=4)
+            return (raw_lo[g], raw_hi[g])[part].rearrange("p j (m t) -> p m j t", t=4)
 
         def quantize_window01(w):
             nc.vector.quantize_mx(codes[w][:].rearrange("p g m -> p (g m)").bitcast(FP8X4),
@@ -140,12 +141,11 @@ def tile_picked_unet_none_p_kernel(tc, x_words, x_scales, w1, w2, skip, offs, ce
 
         skip_rows = skip.rearrange("(p t) v -> p t v", t=4)
         skip_sb = {0: tile("skip0", [P, U], F32, "raw_lo1")}
+        nc.sync.dma_start(win[2][:, U:], skip_rows[:, 3, :])
         nc.sync.dma_start(skip_sb[0][:], skip_rows[:ROWS_HALF, 0:2, :])
         raw_w2 = tile("raw_w2", [P, 4, N], F32, "picked_rows")
         nc.sync.dma_start(raw_w2[:], w2.rearrange("(p j) n -> p j n", j=4))
         pairs = tile("pairs", [P, 2 * U], F32)
-        skip_sb[2] = tile("skip2", [P, U], F32, "xs")
-        nc.sync.dma_start(skip_sb[2][:], skip_rows[:, 2, :])
 
         def product(name, number, w, a, b):
             acc = bank(name, number)[:, : b - a]
@@ -159,10 +159,14 @@ def tile_picked_unet_none_p_kernel(tc, x_words, x_scales, w1, w2, skip, offs, ce
             nc.vector.tensor_copy(win[w][:].indirect(entries(cell_t, a, b)), stage)
 
         stage0 = tile("h_sb0", [P, S], F32)
-        nc.scalar.copy(stage0[:, :SHORT], product("h0_0", 0, 0, 0, SHORT))
-        on_scalar(0, stage0[:, :SHORT], 0, SHORT)
-        nc.scalar.copy(stage0[:, SHORT:HALF], product("h0_1", 1, 0, SHORT, HALF))
-        nc.scalar.copy(stage0[:, HALF:], product("h0_2", 2, 0, HALF, S))
+        first_stage = win[3][:, U : U + SHORT]
+        nc.scalar.copy(first_stage, product("h0_0", 0, 0, 0, SHORT))
+        on_scalar(0, first_stage, 0, SHORT)
+        nc.sync.dma_start(win[3][:, U:], skip_rows[:, 2, :])
+        acc = bank("h0_1", 1)
+        h_product(acc[:, :SHORT], 0, SHORT, HALF)
+        h_product(acc[:, SHORT : S - SHORT], 0, HALF, S)
+        nc.scalar.copy(stage0[:, SHORT:], acc[:, : S - SHORT])
         on_scalar(0, stage0[:, SHORT:], SHORT, S)
         round23(nc.vector.tensor_copy, 0, 1)
         round01(nc.vector.tensor_copy, 0, 1)
@@ -182,13 +186,11 @@ def tile_picked_unet_none_p_kernel(tc, x_words, x_scales, w1, w2, skip, offs, ce
         stage1 = tile("h_sb1", [P, S], F32)
         nc.scalar.copy(stage1[:], product("h1", 5, 1, 0, S))
         nc.vector.tensor_copy(stage2[1][:], product("h2_1", 7, 2, HALF, S))
-        on_vector(2, stage2[1][:], HALF, S)
         stage3 = tile("h_sb3", [P, S], F32)
         nc.scalar.copy(stage3[:], product("h3", 4, 3, 0, S))
+        on_vector(2, stage2[1][:], HALF, S)
         on_scalar(1, stage1[:, :HALF], 0, HALF)
         on_scalar(1, stage1[:, HALF:], HALF, S)
-        skip_sb[3] = tile("skip3", [P, U], F32, "h_sb2_1")
-        nc.sync.dma_start(skip_sb[3][:], skip_rows[:, 3, :])
         w2_bf = tile("w2_bf", [P, N * 4], BF16, "h_sb2_0")
         nc.vector.tensor_copy(
             w2_bf[:].rearrange("p (c n j) -> p c j n", n=4, j=4),
@@ -196,9 +198,6 @@ def tile_picked_unet_none_p_kernel(tc, x_words, x_scales, w1, w2, skip, offs, ce
         )
         w2_codes = tile("w2_codes", [P, N], U32)
         w2_scales = tile("w2_scales", [P, N], U8)
-
-        halves = pairs[:, U:].bitcast(BF16).rearrange("p (v e) -> p v e", e=2)
-        nc.vector.tensor_tensor(halves[:, :, 0], win[2][:], skip_sb[2][:], ADD)
 
         zt_half = [tile(f"zt{hf}", [P, 4, 2 * P], BF16) for hf in range(2)]
         zt = [zt_half[q // 2][:, 2 * (q % 2) : 2 * (q % 2) + 2] for q in range(4)]
@@ -230,16 +229,21 @@ def tile_picked_unet_none_p_kernel(tc, x_words, x_scales, w1, w2, skip, offs, ce
         nc.vector.tensor_copy(win[3][:].indirect(cell_t[:]), stage3[:])
         nc.vector.quantize_mx(w2_codes[:].bitcast(FP8X4), w2_scales[:], w2_bf[:])
         zq = tile("zq", [P, U * 4], BF16, "zt1")
-        edges = (0, SHORT, SHORT + QUARTER, SHORT + 2 * QUARTER, U - 2 * SHORT, U - SHORT, U)
+        edges = (0, QUARTER, 2 * QUARTER, 3 * QUARTER, U - SHORT, U)
         pieces = list(zip(edges[:-1], edges[1:]))
-        for a, b in pieces:
-            nc.vector.tensor_tensor(halves[:, a:b, 1], win[3][:, a:b], skip_sb[3][:, a:b], ADD)
-        for a, b in pieces:
-            nc.scalar.copy(zq[:].bitcast(F32).rearrange("p (v u) -> p v u", u=2)[:, a:b],
-                           pairs[:].rearrange("p (u v) -> p v u", u=2)[:, a:b])
+        sums = pairs[:, U:].bitcast(BF16).rearrange("p (c i e) -> p c e i", i=4, e=2)
+        first = win[2][:].rearrange("p (e c i) -> p c e i", e=2, i=4)
+        second = win[3][:].rearrange("p (e c i) -> p c e i", e=2, i=4)[:, :, ::-1]
+        for a, b in ((0, U // 2), (U // 2, U)):
+            nc.vector.tensor_tensor(sums[:, a // 4 : b // 4], first[:, a // 4 : b // 4], second[:, a // 4 : b // 4], ADD)
+        woven = zq[:].bitcast(F32).rearrange("p (v u) -> p v u", u=2)
+        rows = pairs[:].rearrange("p (u v) -> p v u", u=2)
+        nc.vector.tensor_copy(woven[:, :QUARTER], rows[:, :QUARTER])
+        for a, b in pieces[1:]:
+            nc.scalar.copy(woven[:, a:b], rows[:, a:b])
         banks_out = banks_there + banks_back[:2]
-        res_early = tile("res_early", [P, edges[ON_SCALAR]], F32, "pairs")
-        res_late = tile("res_late", [P, U - edges[ON_SCALAR]], F32)
+        on_scalar_res = tile("res_scalar", [P, U], F32, "pairs")
+        on_vector_res = tile("res_vector", [P, U], F32)
         for n, (a, b) in enumerate(pieces):
             width = b - a
             z_codes = tile(f"z_codes{n}", [P, width], U32)
@@ -248,9 +252,9 @@ def tile_picked_unet_none_p_kernel(tc, x_words, x_scales, w1, w2, skip, offs, ce
             res = bank(f"res{n}", banks_out[n])
             nc.tensor.matmul_mx(res[:, :width], lhsT=w2_codes[:].bitcast(FP8X4), lhsT_scale=w2_scales[:],
                                 rhs=z_codes[:].bitcast(FP8X4), rhs_scale=z_scales[:], start=True, stop=True)
-            if n < ON_SCALAR:
-                nc.scalar.copy(res_early[:, a:b], res[:, :width])
-                (nc.scalar if n == ON_SCALAR - 1 else nc.sync).dma_start(out[:, a:b], res_early[:, a:b])
+            if n in ON_VECTOR:
+                nc.vector.tensor_copy(on_vector_res[:, a:b], res[:, :width])
+                nc.sync.dma_start(out[:, a:b], on_vector_res[:, a:b])
             else:
-                nc.vector.tensor_copy(res_late[:, a - edges[ON_SCALAR] : b - edges[ON_SCALAR]], res[:, :width])
-                nc.sync.dma_start(out[:, a:b], res_late[:, a - edges[ON_SCALAR] : b - edges[ON_SCALAR]])
+                nc.scalar.copy(on_scalar_res[:, a:b], res[:, :width])
+                (nc.scalar if n == len(pieces) - 1 else nc.sync).dma_start(out[:, a:b], on_scalar_res[:, a:b])

@@ -142,9 +142,9 @@ def tile_picked_unet_none_p_kernel(tc, x_words, x_scales, w1, w2, skip, offs, ce
         skip_rows = skip.rearrange("(p t) v -> p t v", t=4)
         skip_sb = {0: tile("skip0", [P, U], F32, "raw_lo1")}
         nc.sync.dma_start(win[2][:, U:], skip_rows[:, 3, :])
-        nc.sync.dma_start(skip_sb[0][:], skip_rows[:ROWS_HALF, 0:2, :])
         raw_w2 = tile("raw_w2", [P, 4, N], F32, "picked_rows")
         nc.sync.dma_start(raw_w2[:], w2.rearrange("(p j) n -> p j n", j=4))
+        nc.sync.dma_start(skip_sb[0][:], skip_rows[:ROWS_HALF, 0:2, :])
         pairs = tile("pairs", [P, 2 * U], F32)
 
         def product(name, number, w, a, b):
@@ -176,26 +176,26 @@ def tile_picked_unet_none_p_kernel(tc, x_words, x_scales, w1, w2, skip, offs, ce
         quantize_half(2, 1, 1)
         round01(nc.vector.tensor_copy, 1, 1)
         quantize_half(3, 1, 1)
-        quantize_window01(1)
         skip_sb[1] = tile("skip1", [P, U], F32, "xw0")
         nc.sync.dma_start(skip_sb[1][:], skip_rows[ROWS_HALF:, 0:2, :])
 
         stage2 = [tile(f"h_sb2_{n}", [P, HALF], F32) for n in range(2)]
         nc.vector.tensor_copy(stage2[0][:], product("h2_0", 3, 2, 0, HALF))
+        quantize_window01(1)
         on_vector(2, stage2[0][:], 0, HALF)
         stage1 = tile("h_sb1", [P, S], F32)
         nc.scalar.copy(stage1[:], product("h1", 5, 1, 0, S))
         nc.vector.tensor_copy(stage2[1][:], product("h2_1", 7, 2, HALF, S))
         stage3 = tile("h_sb3", [P, S], F32)
         nc.scalar.copy(stage3[:], product("h3", 4, 3, 0, S))
-        on_vector(2, stage2[1][:], HALF, S)
-        on_scalar(1, stage1[:, :HALF], 0, HALF)
-        on_scalar(1, stage1[:, HALF:], HALF, S)
         w2_bf = tile("w2_bf", [P, N * 4], BF16, "h_sb2_0")
         nc.vector.tensor_copy(
             w2_bf[:].rearrange("p (c n j) -> p c j n", n=4, j=4),
             raw_w2[:].rearrange("p j (c n) -> p c j n", n=4),
         )
+        on_vector(2, stage2[1][:], HALF, S)
+        on_scalar(1, stage1[:, :HALF], 0, HALF)
+        on_scalar(1, stage1[:, HALF:], HALF, S)
         w2_codes = tile("w2_codes", [P, N], U32)
         w2_scales = tile("w2_scales", [P, N], U8)
 

@@ -26,8 +26,8 @@ SHORT = 128
 QUARTER = U // 4
 RAW = 4 * 2 * P
 ROWS_HALF = P // 2
-MOVES_AHEAD = 3
-ON_VECTOR = (2, 3)
+BLOCKS = 16
+ON_VECTOR = (3,)
 
 
 def tile_picked_unet_none_p_kernel(tc, x_words, x_scales, w1, w2, skip, offs, cell, out):
@@ -48,40 +48,35 @@ def tile_picked_unet_none_p_kernel(tc, x_words, x_scales, w1, w2, skip, offs, ce
         offs_t = sb.tile([P, S // STRIPE], U16, name="offs_t")
         cell_t = sb.tile([P, S // STRIPE], U16, name="cell_t")
         w1_rows = w1.rearrange("(g p j) c -> g p j c", g=PASSES, j=4)
-        xs = tile("xs", [P, T], U8)
-        xw = [tile("xw0", [P, T], U32), tile("xw1", [P, T], U32, "xs")]
+        xs = tile("xs", [P, PASSES * T], U8)
+        xw = [tile("xw0", [P, T], U32), tile("xw1", [P, T], U32)]
         win = [tile(f"win{w}", [P, U * (1 + w // 2)], F32) for w in range(4)]
         raw_lo = [win[2][:, U:], tile("raw_lo1", [P, RAW], F32)[:, :]]
         raw_lo = [r.rearrange("p (j c) -> p j c", j=4) for r in raw_lo]
-        gs = tile("gs", [P, S], U8)
-        nc.vector.memset(xs[32:64, :].bitcast(I32), 0)
-        nc.vector.memset(xs[64:, :].bitcast(I32), 0)
+        gs = tile("gs", [P, PASSES * S], U8)
+        nc.vector.memset(xs[: P - BLOCKS, :].bitcast(I32), 0)
         nc.vector.memset(gs[:].bitcast(I32), 0)
 
         def load_words(g):
             nc.sync.dma_start(xw[g][:].bitcast(I32), x_words[g].rearrange("p n t -> p (n t)").bitcast(I32))
 
         nc.sync.dma_start(offs_t[:], offs)
-        nc.scalar.dma_start(xs[:32, :].bitcast(I32), x_scales.rearrange("g r c -> (g r) c").bitcast(I32))
+        nc.scalar.dma_start(xs[P - BLOCKS :, :].bitcast(I32).rearrange("r (g c) -> r g c", g=PASSES),
+                            x_scales.rearrange("g r c -> r g c").bitcast(I32))
         load_words(0)
-        nc.scalar.dma_start(raw_lo[0], w1_rows[0, :, :, : 2 * P])
-        nc.sync.dma_start(cell_t[:], cell)
-        nc.scalar.dma_start(raw_lo[1], w1_rows[1, :, :, : 2 * P])
+        for g in range(PASSES):
+            nc.sync.dma_start(raw_lo[g], w1_rows[g, :, :, : 2 * P])
 
-        picked_rows = tile("picked_rows", [P, S], U8)
-        nc.vector.tensor_copy(picked_rows[:], xs[:].indirect(offs_t[:]))
-
-        def place_scales(moves):
-            for g, q in moves:
-                src, dst = 16 * g + 4 * q, 32 * q + 4 * g
-                nc.sync.dma_start(gs[dst : dst + 4, :].bitcast(I32), picked_rows[src : src + 4, :].bitcast(I32))
-
-        all_moves = [(g, q) for g in range(PASSES) for q in range(4)]
-        place_scales(all_moves[:MOVES_AHEAD])
         load_words(1)
-        place_scales(all_moves[MOVES_AHEAD:])
+        nc.sync.dma_start(cell_t[:], cell)
+        picked_rows = tile("picked_rows", [P, PASSES * S], U8)
+        for g in range(PASSES):
+            nc.vector.tensor_copy(picked_rows[:, g * S : (g + 1) * S], xs[:, g * T : (g + 1) * T].indirect(offs_t[:]))
+        for q in range(4):
+            src = P - BLOCKS + 4 * q
+            nc.sync.dma_start(gs[32 * q : 32 * q + 4, :].bitcast(I32), picked_rows[src : src + 4, :].bitcast(I32))
 
-        hi_row = tile("hi_row", [P, PASSES * RAW], F32, "xw0")
+        hi_row = tile("hi_row", [P, PASSES * RAW], F32, "xs")
         raw_hi = [hi_row[:, g * RAW : (g + 1) * RAW].rearrange("p (j c) -> p j c", j=4) for g in range(PASSES)]
         for g in range(PASSES):
             nc.sync.dma_start(raw_hi[g], w1_rows[g, :, :, 2 * P :])
@@ -126,7 +121,7 @@ def tile_picked_unet_none_p_kernel(tc, x_words, x_scales, w1, w2, skip, offs, ce
                     lhsT=codes[w][:, g].bitcast(FP8X4),
                     lhsT_scale=scales[w][:, g],
                     rhs=gw[g][:, a:b].bitcast(FP8X4),
-                    rhs_scale=gs[4 * g :, a:b],
+                    rhs_scale=gs[:, g * S + a : g * S + b],
                     start=(g == 0),
                     stop=(g == PASSES - 1),
                 )
@@ -176,16 +171,19 @@ def tile_picked_unet_none_p_kernel(tc, x_words, x_scales, w1, w2, skip, offs, ce
         quantize_half(2, 1, 1)
         round01(nc.vector.tensor_copy, 1, 1)
         quantize_half(3, 1, 1)
-        skip_sb[1] = tile("skip1", [P, U], F32, "xw0")
+        skip_sb[1] = tile("skip1", [P, U], F32, "xs")
         nc.sync.dma_start(skip_sb[1][:], skip_rows[ROWS_HALF:, 0:2, :])
 
         stage2 = [tile(f"h_sb2_{n}", [P, HALF], F32) for n in range(2)]
         nc.vector.tensor_copy(stage2[0][:], product("h2_0", 3, 2, 0, HALF))
         quantize_window01(1)
         on_vector(2, stage2[0][:], 0, HALF)
+        nc.scalar.copy(stage2[1][:], product("h2_1", 7, 2, HALF, S))
         stage1 = tile("h_sb1", [P, S], F32)
-        nc.scalar.copy(stage1[:], product("h1", 5, 1, 0, S))
-        nc.vector.tensor_copy(stage2[1][:], product("h2_1", 7, 2, HALF, S))
+        acc = product("h1", 5, 1, 0, S)
+        nc.scalar.copy(stage1[:, :SHORT], acc[:, :SHORT])
+        nc.scalar.copy(stage1[:, SHORT:], acc[:, SHORT:])
+        on_scalar(1, stage1[:, :SHORT], 0, SHORT)
         stage3 = tile("h_sb3", [P, S], F32)
         nc.scalar.copy(stage3[:], product("h3", 4, 3, 0, S))
         w2_bf = tile("w2_bf", [P, N * 4], BF16, "h_sb2_0")
@@ -194,8 +192,7 @@ def tile_picked_unet_none_p_kernel(tc, x_words, x_scales, w1, w2, skip, offs, ce
             raw_w2[:].rearrange("p j (c n) -> p c j n", n=4),
         )
         on_vector(2, stage2[1][:], HALF, S)
-        on_scalar(1, stage1[:, :HALF], 0, HALF)
-        on_scalar(1, stage1[:, HALF:], HALF, S)
+        on_scalar(1, stage1[:, SHORT:], SHORT, S)
         w2_codes = tile("w2_codes", [P, N], U32)
         w2_scales = tile("w2_scales", [P, N], U8)
 
@@ -208,27 +205,34 @@ def tile_picked_unet_none_p_kernel(tc, x_words, x_scales, w1, w2, skip, offs, ce
                                  rhs=ident[:], is_transpose=True,
                                  start=(opening and n == 0), stop=(not opening and n == len(blocks) - 1))
 
+        totals0 = [bank(f"z0_{hf}", 5 + hf) for hf in range(2)]
         for hf in range(2):
-            total = bank(f"z0_{hf}", 5 + hf)
-            add_transposed(total, skip_sb[0], range(4 * hf, 4 * hf + 4), True)
-            add_transposed(total, win[0], range(4 * hf, 4 * hf + 4), False)
-            nc.scalar.copy(zt_half[hf][:, :, :P], total[:].rearrange("p (c x) -> p c x", c=4))
+            add_transposed(totals0[hf], skip_sb[0], range(4 * hf, 4 * hf + 4), True)
+            add_transposed(totals0[hf], win[0], range(4 * hf, 4 * hf + 4), False)
         banks_there, banks_back = (0, 1, 2, 3), (7, 4, 5, 6)
         totals = [bank(f"z1_{q}", banks_there[q]) for q in range(4)]
         for q in range(4):
             add_transposed(totals[q], skip_sb[1], (2 * q, 2 * q + 1), True)
         for q in range(4):
             add_transposed(totals[q], win[1], (2 * q, 2 * q + 1), False)
-            nc.scalar.copy(zt[q][:, :, P:], totals[q][:, :QUARTER].rearrange("p (c x) -> p c x", c=2))
-        for q in range(4):
+
+        def turn_back(q):
             back = bank(f"back{q}", banks_back[q])
             for c in range(2):
                 nc.tensor.transpose(back[:, c * P : (c + 1) * P], zt[q][:, c, :].bitcast(F32), ident[:])
             nc.scalar.copy(pairs[:, q * QUARTER : (q + 1) * QUARTER], back[:, :QUARTER])
 
+        for q in range(4):
+            if q % 2 == 0:
+                nc.scalar.copy(zt_half[q // 2][:, :, :P], totals0[q // 2][:].rearrange("p (c x) -> p c x", c=4))
+            nc.scalar.copy(zt[q][:, :, P:], totals[q][:, :QUARTER].rearrange("p (c x) -> p c x", c=2))
+            if q > 0:
+                turn_back(q - 1)
+        turn_back(3)
+
         nc.vector.tensor_copy(win[3][:].indirect(cell_t[:]), stage3[:])
         nc.vector.quantize_mx(w2_codes[:].bitcast(FP8X4), w2_scales[:], w2_bf[:])
-        zq = tile("zq", [P, U * 4], BF16, "zt1")
+        zq = [tile("zq_first", [P, U * 2], BF16), tile("zq_second", [P, U * 2], BF16, "zt1")]
         edges = (0, QUARTER, 2 * QUARTER, 3 * QUARTER, U - SHORT, U)
         pieces = list(zip(edges[:-1], edges[1:]))
         sums = pairs[:, U:].bitcast(BF16).rearrange("p (c i e) -> p c e i", i=4, e=2)
@@ -236,11 +240,12 @@ def tile_picked_unet_none_p_kernel(tc, x_words, x_scales, w1, w2, skip, offs, ce
         second = win[3][:].rearrange("p (e c i) -> p c e i", e=2, i=4)[:, :, ::-1]
         for a, b in ((0, U // 2), (U // 2, U)):
             nc.vector.tensor_tensor(sums[:, a // 4 : b // 4], first[:, a // 4 : b // 4], second[:, a // 4 : b // 4], ADD)
-        woven = zq[:].bitcast(F32).rearrange("p (v u) -> p v u", u=2)
+        woven = [z[:].bitcast(F32).rearrange("p (v u) -> p v u", u=2) for z in zq]
         rows = pairs[:].rearrange("p (u v) -> p v u", u=2)
-        nc.vector.tensor_copy(woven[:, :QUARTER], rows[:, :QUARTER])
-        for a, b in pieces[1:]:
-            nc.scalar.copy(woven[:, a:b], rows[:, a:b])
+        for a, b in pieces[:2]:
+            nc.vector.tensor_copy(woven[0][:, a:b], rows[:, a:b])
+        for a, b in pieces[2:]:
+            nc.scalar.copy(woven[1][:, a - U // 2 : b - U // 2], rows[:, a:b])
         banks_out = banks_there + banks_back[:2]
         on_scalar_res = tile("res_scalar", [P, U], F32, "pairs")
         on_vector_res = tile("res_vector", [P, U], F32)
@@ -248,7 +253,7 @@ def tile_picked_unet_none_p_kernel(tc, x_words, x_scales, w1, w2, skip, offs, ce
             width = b - a
             z_codes = tile(f"z_codes{n}", [P, width], U32)
             z_scales = tile(f"z_scales{n}", [P, width], U8)
-            nc.vector.quantize_mx(z_codes[:].bitcast(FP8X4), z_scales[:], zq[:, 4 * a : 4 * b])
+            nc.vector.quantize_mx(z_codes[:].bitcast(FP8X4), z_scales[:], zq[a // (U // 2)][:, 4 * (a % (U // 2)) : 4 * (a % (U // 2) + width)])
             res = bank(f"res{n}", banks_out[n])
             nc.tensor.matmul_mx(res[:, :width], lhsT=w2_codes[:].bitcast(FP8X4), lhsT_scale=w2_scales[:],
                                 rhs=z_codes[:].bitcast(FP8X4), rhs_scale=z_scales[:], start=True, stop=True)

@@ -179,20 +179,20 @@ def tile_picked_unet_none_p_kernel(tc, x_words, x_scales, w1, w2, skip, offs, ce
         quantize_window01(1)
         on_vector(2, stage2[0][:], 0, HALF)
         nc.scalar.copy(stage2[1][:], product("h2_1", 7, 2, HALF, S))
-        stage1 = tile("h_sb1", [P, S], F32)
-        acc = product("h1", 5, 1, 0, S)
-        nc.scalar.copy(stage1[:, :SHORT], acc[:, :SHORT])
-        nc.scalar.copy(stage1[:, SHORT:], acc[:, SHORT:])
-        on_scalar(1, stage1[:, :SHORT], 0, SHORT)
         stage3 = tile("h_sb3", [P, S], F32)
         nc.scalar.copy(stage3[:], product("h3", 4, 3, 0, S))
+        stage1 = tile("h_sb1", [P, S], F32)
+        acc = product("h1", 5, 1, 0, S)
+        nc.scalar.copy(stage1[:, :HALF], acc[:, :HALF])
+        nc.scalar.copy(stage1[:, HALF:], acc[:, HALF:])
+        on_scalar(1, stage1[:, :HALF], 0, HALF)
         w2_bf = tile("w2_bf", [P, N * 4], BF16, "h_sb2_0")
         nc.vector.tensor_copy(
             w2_bf[:].rearrange("p (c n j) -> p c j n", n=4, j=4),
             raw_w2[:].rearrange("p j (c n) -> p c j n", n=4),
         )
         on_vector(2, stage2[1][:], HALF, S)
-        on_scalar(1, stage1[:, SHORT:], SHORT, S)
+        on_scalar(1, stage1[:, HALF:], HALF, S)
         w2_codes = tile("w2_codes", [P, N], U32)
         w2_scales = tile("w2_scales", [P, N], U8)
 
@@ -205,11 +205,11 @@ def tile_picked_unet_none_p_kernel(tc, x_words, x_scales, w1, w2, skip, offs, ce
                                  rhs=ident[:], is_transpose=True,
                                  start=(opening and n == 0), stop=(not opening and n == len(blocks) - 1))
 
-        totals0 = [bank(f"z0_{hf}", 5 + hf) for hf in range(2)]
+        totals0 = [bank(f"z0_{hf}", (7, 4)[hf]) for hf in range(2)]
         for hf in range(2):
             add_transposed(totals0[hf], skip_sb[0], range(4 * hf, 4 * hf + 4), True)
             add_transposed(totals0[hf], win[0], range(4 * hf, 4 * hf + 4), False)
-        banks_there, banks_back = (0, 1, 2, 3), (7, 4, 5, 6)
+        banks_there, banks_back = (0, 1, 2, 3), (5, 6, 7, 4)
         totals = [bank(f"z1_{q}", banks_there[q]) for q in range(4)]
         for q in range(4):
             add_transposed(totals[q], skip_sb[1], (2 * q, 2 * q + 1), True)

@@ -27,7 +27,7 @@ QUARTER = U // 4
 RAW = 4 * 2 * P
 ROWS_HALF = P // 2
 BLOCKS = 16
-ON_VECTOR = (3,)
+ON_VECTOR = (2, 3)
 
 
 def tile_picked_unet_none_p_kernel(tc, x_words, x_scales, w1, w2, skip, offs, cell, out):
@@ -178,7 +178,7 @@ def tile_picked_unet_none_p_kernel(tc, x_words, x_scales, w1, w2, skip, offs, ce
         nc.vector.tensor_copy(stage2[0][:], product("h2_0", 3, 2, 0, HALF))
         quantize_window01(1)
         on_vector(2, stage2[0][:], 0, HALF)
-        nc.scalar.copy(stage2[1][:], product("h2_1", 7, 2, HALF, S))
+        nc.vector.tensor_copy(stage2[1][:], product("h2_1", 7, 2, HALF, S))
         stage3 = tile("h_sb3", [P, S], F32)
         nc.scalar.copy(stage3[:], product("h3", 4, 3, 0, S))
         stage1 = tile("h_sb1", [P, S], F32)

@@ -130,7 +130,7 @@ def tile_picked_unet_none_p_kernel(tc, x_words, x_scales, w1, w2, skip, offs, ce
             round01(nc.scalar.copy, g, 0)
         quantize_window01(0)
         for g in range(PASSES):
-            round23(nc.scalar.copy, g, 0)
+            round23(nc.vector.tensor_copy, g, 0)
             for w in (2, 3):
                 quantize_half(w, g, 0)
 

from contextlib import ExitStack

import concourse.mybir as mybir
from concourse.masks import make_identity

K, T, S, H, N, U = 1024, 2048, 512, 512, 128, 1024
FLOPS = 2 * K * H * S + 2 * H * N * U

F32 = mybir.dt.float32
BF16 = mybir.dt.bfloat16
I32 = mybir.dt.int32
U32 = mybir.dt.uint32
U16 = mybir.dt.uint16
U8 = mybir.dt.uint8
FP8X4 = mybir.dt.float8_e4m3fn_x4
ADD = mybir.AluOpType.add
COPY = mybir.ActivationFunctionType.Copy

P = 128
PASSES = K // 512
BANK = 512
ALIGN = 64
STRIPE = 16
HALF = S // 2
SHORT = 128
QUARTER = U // 4
RAW = 4 * 2 * P
ROWS_HALF = P // 2
BLOCKS = 16
ON_VECTOR = (2, 3)


def tile_picked_unet_none_p_kernel(tc, x_words, x_scales, w1, w2, skip, offs, cell, out):
    nc = tc.nc
    with ExitStack() as ctx:
        sb = ctx.enter_context(tc.tile_pool(name="sb", bufs=1))
        ps = ctx.enter_context(tc.psum_pool(name="ps", bufs=1))

        def tile(name, shape, dtype, tag=None):
            return sb.tile(shape, dtype, name=name, tag=tag or name, align_bytes=ALIGN)

        def bank(name, number):
            return ps.tile([P, BANK], F32, name=name, tag=f"B{number}")

        def entries(list_tile, a, b):
            return list_tile[:, a // STRIPE : b // STRIPE]

        offs_t = sb.tile([P, S // STRIPE], U16, name="offs_t")
        cell_t = sb.tile([P, S // STRIPE], U16, name="cell_t")
        w1_rows = w1.rearrange("(g p j) c -> g p j c", g=PASSES, j=4)
        xs = tile("xs", [P, PASSES * T], U8)
        xw = [tile("xw0", [P, T], U32), tile("xw1", [P, T], U32)]
        win = [tile(f"win{w}", [P, U * (1 + w // 2)], F32) for w in range(4)]
        raw_lo = [win[2][:, U:], tile("raw_lo1", [P, RAW], F32)[:, :]]
        raw_lo = [r.rearrange("p (j c) -> p j c", j=4) for r in raw_lo]
        gs = tile("gs", [P, PASSES * S], U8)
        nc.vector.memset(xs[: P - BLOCKS, :].bitcast(I32), 0)
        nc.vector.memset(gs[:].bitcast(I32), 0)

        def load_words(g):
            nc.sync.dma_start(xw[g][:].bitcast(I32), x_words[g].rearrange("p n t -> p (n t)").bitcast(I32))

        nc.sync.dma_start(offs_t[:], offs)
        nc.scalar.dma_start(xs[P - BLOCKS :, :].bitcast(I32).rearrange("r (g c) -> r g c", g=PASSES),
                            x_scales.rearrange("g r c -> r g c").bitcast(I32))
        load_words(0)
        for g in range(PASSES):
            nc.sync.dma_start(raw_lo[g], w1_rows[g, :, :, : 2 * P])

        load_words(1)
        nc.sync.dma_start(cell_t[:], cell)
        picked_rows = tile("picked_rows", [P, PASSES * S], U8)
        for g in range(PASSES):
            nc.vector.tensor_copy(picked_rows[:, g * S : (g + 1) * S], xs[:, g * T : (g + 1) * T].indirect(offs_t[:]))
        for q in range(4):
            src = P - BLOCKS + 4 * q
            nc.sync.dma_start(gs[32 * q : 32 * q + 4, :].bitcast(I32), picked_rows[src : src + 4, :].bitcast(I32))

        hi_row = tile("hi_row", [P, PASSES * RAW], F32, "xs")
        raw_hi = [hi_row[:, g * RAW : (g + 1) * RAW].rearrange("p (j c) -> p j c", j=4) for g in range(PASSES)]
        for g in range(PASSES):
            nc.sync.dma_start(raw_hi[g], w1_rows[g, :, :, 2 * P :])
        ident = tile("ident", [P, P], F32)
        make_identity(nc, ident[:])
        nc.vector.memset(win[0][:], 0.0)
        for w in (2, 1, 3):
            nc.scalar.copy(win[w][:, :U], win[0][:])

        gw = [tile(f"gw{g}", [P, S], U32) for g in range(PASSES)]
        nc.vector.tensor_copy(gw[0][:], xw[0][:].indirect(offs_t[:]))
        for a, b in ((0, SHORT), (SHORT, HALF), (HALF, S)):
            nc.vector.tensor_copy(gw[1][:, a:b], xw[1][:].indirect(entries(offs_t, a, b)))

        bf23 = tile("w1_bf23", [P, 2, PASSES, P * 4], BF16)
        bf = [tile(f"w1_bf{w}", [P, PASSES, P * 4], BF16)[:, :, :] for w in range(2)] + [bf23[:, u] for u in range(2)]
        codes = [tile(f"w1_codes{w}", [P, PASSES, P], U32) for w in range(4)]
        scales = [tile(f"w1_scales{w}", [P, PASSES, P], U8) for w in range(4)]

        def raw_part(g, part):
            return (raw_lo[g], raw_hi[g])[part].rearrange("p j (m t) -> p m j t", t=4)

        def quantize_window01(w):
            nc.vector.quantize_mx(codes[w][:].rearrange("p g m -> p (g m)").bitcast(FP8X4),
                                  scales[w][:].rearrange("p g m -> p (g m)"), bf[w].rearrange("p g x -> p (g x)"))

        def round01(copy, g, part):
            copy(bf[part][:, g].rearrange("p (m e j) -> p m j e", e=2, j=4), raw_part(g, part)[:, :, :, 0:2])

        def round23(copy, g, part):
            a, b = ROWS_HALF * part, ROWS_HALF * (part + 1)
            copy(bf23[:, :, g].rearrange("p u (m j) -> p m j u", j=4)[:, a:b], raw_part(g, part)[:, :, :, 2:4])

        def quantize_half(w, g, part):
            a, b = ROWS_HALF * part, ROWS_HALF * (part + 1)
            nc.vector.quantize_mx(codes[w][:, g, a:b].bitcast(FP8X4), scales[w][:, g, a:b], bf[w][:, g, 4 * a : 4 * b])

        def h_product(acc, w, a, b):
            for g in range(PASSES):
                nc.tensor.matmul_mx(
                    acc,
                    lhsT=codes[w][:, g].bitcast(FP8X4),
                    lhsT_scale=scales[w][:, g],
                    rhs=gw[g][:, a:b].bitcast(FP8X4),
                    rhs_scale=gs[:, g * S + a : g * S + b],
                    start=(g == 0),
                    stop=(g == PASSES - 1),
                )

        for g in range(PASSES):
            round01(nc.scalar.copy, g, 0)
        quantize_window01(0)
        for g in range(PASSES):
            round23(nc.vector.tensor_copy, g, 0)
            for w in (2, 3):
                quantize_half(w, g, 0)

        skip_rows = skip.rearrange("(p t) v -> p t v", t=4)
        skip_sb = {0: tile("skip0", [P, U], F32, "raw_lo1")}
        nc.sync.dma_start(win[2][:, U:], skip_rows[:, 3, :])
        raw_w2 = tile("raw_w2", [P, 4, N], F32, "picked_rows")
        nc.sync.dma_start(raw_w2[:], w2.rearrange("(p j) n -> p j n", j=4))
        nc.sync.dma_start(skip_sb[0][:], skip_rows[:ROWS_HALF, 0:2, :])
        pairs = tile("pairs", [P, 2 * U], F32)

        def product(name, number, w, a, b):
            acc = bank(name, number)[:, : b - a]
            h_product(acc, w, a, b)
            return acc

        def on_scalar(w, stage, a, b):
            nc.scalar.activation(win[w][:].indirect(entries(cell_t, a, b)), stage, COPY)

        def on_vector(w, stage, a, b):
            nc.vector.tensor_copy(win[w][:].indirect(entries(cell_t, a, b)), stage)

        stage0 = tile("h_sb0", [P, S], F32)
        first_stage = win[3][:, U : U + SHORT]
        nc.scalar.copy(first_stage, product("h0_0", 0, 0, 0, SHORT))
        on_scalar(0, first_stage, 0, SHORT)
        nc.sync.dma_start(win[3][:, U:], skip_rows[:, 2, :])
        acc = bank("h0_1", 1)
        h_product(acc[:, :SHORT], 0, SHORT, HALF)
        h_product(acc[:, SHORT : S - SHORT], 0, HALF, S)
        nc.scalar.copy(stage0[:, SHORT:], acc[:, : S - SHORT])
        on_scalar(0, stage0[:, SHORT:], SHORT, S)
        round23(nc.vector.tensor_copy, 0, 1)
        round01(nc.vector.tensor_copy, 0, 1)
        quantize_half(2, 0, 1)
        round23(nc.vector.tensor_copy, 1, 1)
        quantize_half(3, 0, 1)
        quantize_half(2, 1, 1)
        round01(nc.vector.tensor_copy, 1, 1)
        quantize_half(3, 1, 1)
        skip_sb[1] = tile("skip1", [P, U], F32, "xs")
        nc.sync.dma_start(skip_sb[1][:], skip_rows[ROWS_HALF:, 0:2, :])

        stage2 = [tile(f"h_sb2_{n}", [P, HALF], F32) for n in range(2)]
        nc.vector.tensor_copy(stage2[0][:], product("h2_0", 3, 2, 0, HALF))
        quantize_window01(1)
        on_vector(2, stage2[0][:], 0, HALF)
        nc.vector.tensor_copy(stage2[1][:], product("h2_1", 7, 2, HALF, S))
        stage3 = tile("h_sb3", [P, S], F32)
        nc.scalar.copy(stage3[:], product("h3", 4, 3, 0, S))
        stage1 = tile("h_sb1", [P, S], F32)
        acc = product("h1", 5, 1, 0, S)
        nc.scalar.copy(stage1[:, :HALF], acc[:, :HALF])
        nc.scalar.copy(stage1[:, HALF:], acc[:, HALF:])
        on_scalar(1, stage1[:, :HALF], 0, HALF)
        w2_bf = tile("w2_bf", [P, N * 4], BF16, "h_sb2_0")
        nc.vector.tensor_copy(
            w2_bf[:].rearrange("p (c n j) -> p c j n", n=4, j=4),
            raw_w2[:].rearrange("p j (c n) -> p c j n", n=4),
        )
        on_vector(2, stage2[1][:], HALF, S)
        on_scalar(1, stage1[:, HALF:], HALF, S)
        w2_codes = tile("w2_codes", [P, N], U32)
        w2_scales = tile("w2_scales", [P, N], U8)

        zt_half = [tile(f"zt{hf}", [P, 4, 2 * P], BF16) for hf in range(2)]
        zt = [zt_half[q // 2][:, 2 * (q % 2) : 2 * (q % 2) + 2] for q in range(4)]

        def add_transposed(total, source, blocks, opening):
            for n, c in enumerate(blocks):
                nc.tensor.matmul(total[:, n * P : (n + 1) * P], lhsT=source[:, c * P : (c + 1) * P],
                                 rhs=ident[:], is_transpose=True,
                                 start=(opening and n == 0), stop=(not opening and n == len(blocks) - 1))

        totals0 = [bank(f"z0_{hf}", (7, 4)[hf]) for hf in range(2)]
        for hf in range(2):
            add_transposed(totals0[hf], skip_sb[0], range(4 * hf, 4 * hf + 4), True)
            add_transposed(totals0[hf], win[0], range(4 * hf, 4 * hf + 4), False)
        banks_there, banks_back = (0, 1, 2, 3), (5, 6, 7, 4)
        totals = [bank(f"z1_{q}", banks_there[q]) for q in range(4)]
        for q in range(4):
            add_transposed(totals[q], skip_sb[1], (2 * q, 2 * q + 1), True)
        for q in range(4):
            add_transposed(totals[q], win[1], (2 * q, 2 * q + 1), False)

        def turn_back(q):
            back = bank(f"back{q}", banks_back[q])
            for c in range(2):
                nc.tensor.transpose(back[:, c * P : (c + 1) * P], zt[q][:, c, :].bitcast(F32), ident[:])
            nc.scalar.copy(pairs[:, q * QUARTER : (q + 1) * QUARTER], back[:, :QUARTER])

        for q in range(4):
            if q % 2 == 0:
                nc.scalar.copy(zt_half[q // 2][:, :, :P], totals0[q // 2][:].rearrange("p (c x) -> p c x", c=4))
            nc.scalar.copy(zt[q][:, :, P:], totals[q][:, :QUARTER].rearrange("p (c x) -> p c x", c=2))
            if q > 0:
                turn_back(q - 1)
        turn_back(3)

        nc.vector.tensor_copy(win[3][:].indirect(cell_t[:]), stage3[:])
        nc.vector.quantize_mx(w2_codes[:].bitcast(FP8X4), w2_scales[:], w2_bf[:])
        zq = [tile("zq_first", [P, U * 2], BF16), tile("zq_second", [P, U * 2], BF16, "zt1")]
        edges = (0, QUARTER, 2 * QUARTER, 3 * QUARTER, U - SHORT, U)
        pieces = list(zip(edges[:-1], edges[1:]))
        sums = pairs[:, U:].bitcast(BF16).rearrange("p (c i e) -> p c e i", i=4, e=2)
        first = win[2][:].rearrange("p (e c i) -> p c e i", e=2, i=4)
        second = win[3][:].rearrange("p (e c i) -> p c e i", e=2, i=4)[:, :, ::-1]
        for a, b in ((0, U // 2), (U // 2, U)):
            nc.vector.tensor_tensor(sums[:, a // 4 : b // 4], first[:, a // 4 : b // 4], second[:, a // 4 : b // 4], ADD)
        woven = [z[:].bitcast(F32).rearrange("p (v u) -> p v u", u=2) for z in zq]
        rows = pairs[:].rearrange("p (u v) -> p v u", u=2)
        for a, b in pieces[:2]:
            nc.vector.tensor_copy(woven[0][:, a:b], rows[:, a:b])
        for a, b in pieces[2:]:
            nc.scalar.copy(woven[1][:, a - U // 2 : b - U // 2], rows[:, a:b])
        banks_out = banks_there + banks_back[:2]
        on_scalar_res = tile("res_scalar", [P, U], F32, "pairs")
        on_vector_res = tile("res_vector", [P, U], F32)
        for n, (a, b) in enumerate(pieces):
            width = b - a
            z_codes = tile(f"z_codes{n}", [P, width], U32)
            z_scales = tile(f"z_scales{n}", [P, width], U8)
            nc.vector.quantize_mx(z_codes[:].bitcast(FP8X4), z_scales[:], zq[a // (U // 2)][:, 4 * (a % (U // 2)) : 4 * (a % (U // 2) + width)])
            res = bank(f"res{n}", banks_out[n])
            nc.tensor.matmul_mx(res[:, :width], lhsT=w2_codes[:].bitcast(FP8X4), lhsT_scale=w2_scales[:],
                                rhs=z_codes[:].bitcast(FP8X4), rhs_scale=z_scales[:], start=True, stop=True)
            if n in ON_VECTOR:
                nc.vector.tensor_copy(on_vector_res[:, a:b], res[:, :width])
                nc.sync.dma_start(out[:, a:b], on_vector_res[:, a:b])
            else:
                nc.scalar.copy(on_scalar_res[:, a:b], res[:, :width])
                (nc.scalar if n == len(pieces) - 1 else nc.sync).dma_start(out[:, a:b], on_scalar_res[:, a:b])
